import numpy as np, ml_dtypes
CORES = [16,18,20,22]
N = 4
import mx_ref
BF = ml_dtypes.bfloat16
def gentries(a):
    return np.ascontiguousarray(a.reshape(8, 16, -1).transpose(0, 2, 1)).reshape(8, -1)
def gtable(e):
    e = np.asarray(e); return np.ascontiguousarray(e.reshape(8, -1, 16).transpose(0, 2, 1)).reshape(128, -1).astype(np.int32)
def gcols(t, e):
    v = np.concatenate([t.reshape(8, 16, -1, 4), np.zeros((8, 16, 1, 4), BF)], axis=2)
    return np.ascontiguousarray(np.stack([v[g][:, e[g]] for g in range(8)])).reshape(128, -1)
def tile(rs):
    return np.stack(rs, axis=2).reshape(128, -1).astype(BF)
def pick(q, e):
    c = np.concatenate([q[0].reshape(128, -1, 4), np.zeros((128, 1, 4), np.uint8)], axis=1); s = np.concatenate([q[1], np.ones((16, 1), np.uint8)], axis=1)
    return (np.ascontiguousarray(c[:, e].reshape(128, -1)), np.ascontiguousarray(s[:, e]))
def join(*qs):
    return (np.concatenate([q[0] for q in qs], axis=1), np.concatenate([q[1] for q in qs], axis=1))
def put(q, e, v):
    c, s = q[0].reshape(128, -1, 4).copy(), q[1].copy(); c[:, e] = v[0].reshape(128, -1, 4); s[:, e] = v[1]
    return (c.reshape(128, -1), s)
def pk(c, s):
    return (np.ascontiguousarray(c), mx_ref.live(s))
def emit(q):
    return q[0], q[1]
def packed(v, rng):
    q = [mx_ref.quantize(np.ascontiguousarray(v[r])) for r in range(N)]
    return np.stack([a for a, b in q]), np.stack([mx_ref.plane(b, rng) for a, b in q])
def values_of_codes():
    e, c = np.zeros((128, 128, 4), np.float32), np.zeros((128, 2, 4), np.uint8)
    e[np.arange(128), np.arange(128), 0] = 1
    c[:127, :, 0] = np.arange(256).reshape(2, 128).T[:127]
    return mx_ref.matmul(mx_ref.quantize(e.reshape(128, 512).astype(BF)), (c.reshape(128, 8), np.full((16, 2), 127, np.uint8))).T.reshape(-1).astype(np.float64)
CODE_VALUE, SCALE_VALUE = values_of_codes(), 2.0 ** (np.arange(256) - 127.0)
def decode(q):
    return (CODE_VALUE[q[0]].reshape(16, 8, -1, 4) * SCALE_VALUE[q[1]][:, None, :, None] + 0.0).reshape(128, -1).astype(np.float32)
def f(rng, *shape):
    return mx_ref.flush((rng.standard_normal(shape, dtype=np.float32) * np.exp2(rng.integers(-2, 3, shape[:-1] + (1,)))).astype(BF))
def wide(rng, *shape, cols=0):
    v = rng.standard_normal(shape, dtype=np.float32) * np.exp2(rng.integers(-12, 13, shape)).astype(np.float32)
    if cols: v *= np.repeat(np.exp2(rng.integers(-cols, cols + 1, shape[:-2] + (1, shape[-1] // 4))) * (rng.random(shape[:-2] + (1, shape[-1] // 4)) > 0.0625), 4, axis=-1).astype(np.float32)
    return mx_ref.flush(v.astype(BF))
C = 384
STEP = [1, 2, 3]
def numbers_of(rng):
    return {"x": np.array(f(rng, N, 128, 4 * C)), "u": np.array(f(rng, N, 128, 512)), "v": np.array(f(rng, N, 128, 512))}
def stored(w):
    return {"wl": np.stack([gtable(w[r]) for r in range(N)])}
def joined(k):
    w = np.zeros_like(k)
    np.put_along_axis(w, k[..., 0::2], k[..., 1::2], axis=-1)
    np.put_along_axis(w, k[..., 1::2], k[..., 0::2], axis=-1)
    return w
def wiring(rng):
    return stored(joined(rng.permuted(np.tile(np.arange(3 * C), (N, 8, 1)), axis=2)))
def edges(rng):
    w = np.zeros((N, 8, 3 * C), np.int64)
    c, i = np.arange(C), np.arange(3 * C)
    for r in range(N):
        a = C + rng.permutation(2 * C)
        k = [i ^ 1, 3 * C - 1 - i, (i + 3 * (C // 2)) % (3 * C), np.concatenate([c + C, c, (c ^ 1) + 2 * C]), np.concatenate([C - 1 - c, c + 2 * C, c + C]),
             joined(np.concatenate([rng.permutation(C), C + rng.permutation(2 * C)])), joined(np.concatenate([np.stack([c, a[:C]], axis=1).reshape(-1), a[C:]])), joined(rng.permutation(3 * C))]
        w[r, rng.permutation(8)] = np.stack(k)
    return stored(w)
def layers(rng):
    return np.array(f(rng, N, 128, 2048)).reshape(N, 8, 16, 4, 8, 16, 4)
def weights(rng, w):
    c, p = packed(np.ascontiguousarray(w).reshape(N, 128, 2048), rng)
    return {"wc": c, "ws": p}
def blank(d):
    u = d["u"].reshape(N, 128, 128, 4)
    u[:, :, 0::16] = 0
    u[:, :, 1::16] = 0
    return u
def setup_inputs(rng):
    return {**numbers_of(rng), **wiring(rng), **weights(rng, layers(rng))}
def setup_inputs_ties(rng):
    d = numbers_of(rng)
    o = rng.permutation(N)
    k = rng.integers(-1, 2, (N, 8, 2, C)).astype(np.float32)
    k[o[1]] = 1
    x = d["x"].reshape(N, 8, 16, C, 4)
    x[:, :, :3] = 0
    x[:, :, :2, :, 0] = k.astype(BF)
    x[:, :, 2, :, 0] = 1.96875 * 2.0 ** 7
    x[:, :, 3] = (np.array([9.0, 11.0, 5.0, 7.0]) * 2.0 ** -9).astype(np.float32).astype(BF)
    a = np.exp2(rng.integers(-3, 4, (1, 8, 1)).astype(np.float32))
    x[:, :, 8:] = 0
    x[:, :, 8, :, 0] = (-1.125 * a).astype(BF)
    x[:, :, 10, :, 0] = (-0.0703125 * a).astype(BF)
    c = np.ones(N, np.float32)
    c[o[0]] = 0
    c[o[2]] = -1
    u = blank(d)
    for h in range(0, 128, 16):
        for i in range(2): u[:, h + i, h + i, 0] = c.astype(BF)
    w = layers(rng)
    w[:, :, 2] = 0
    w[:, :, :, :, :, :4] = 0
    w[:, :, :, :, :, 8:] = 0
    for g in range(8):
        w[:, g, 8, 0, g, 8, 0] = -28.0
        for b in range(4):
            w[:, g, 10, b, g, 9, 0] = -2.0 ** (b - 5)
            w[:, g, 3, b, g, 3, b] = 64.0
    return {"x": x.reshape(N, 128, 4 * C), "u": u.reshape(N, 128, 512), "v": d["v"], **wiring(rng), **weights(rng, w)}
def setup_inputs_near(rng):
    d = numbers_of(rng)
    o = np.zeros(N, np.int64)
    for i, r in enumerate(rng.permutation([r for r in range(N) if r < (r ^ STEP[0])])):
        o[[r, r ^ STEP[0]]] = rng.permutation([0, 3] if i % 2 == 0 else [1, 2])
    x = d["x"].astype(np.float32).reshape(N, 8, 16, C, 4)
    x[:, :, :8] = 0
    u = blank(d)
    at = [0, C - 1, int(rng.integers(C)), int(rng.integers(C))]
    for r in range(N):
        s = rng.integers(-1, 2, (2, 8, C)).astype(np.float32)
        k = 2.0 ** -30 if o[r] in (0, 3) else 1.0
        for i in range(2):
            if o[r] == 2: x[r, :, 2 * i, :, 0] = s[i] * 2.0 ** -8
            else:
                x[r, :, 2 * i, :, 0] = 1.125 * k * s[i]
                x[r, :, 2 * i + 1, :, 0] = -1.25 * k * s[i]
                for g, j in zip(rng.permutation(8)[:4], at): x[r, g, 2 * i, j, 0] = 2.0 ** 30 * rng.choice([-1.0, 1.0])
            for h in range(0, 128, 16):
                u[r, h + 2 * i, h + i, 0] = 1.125 * k
                u[r, h + 2 * i + 1, h + i, 0] = k
        if o[r] == 2: x[r, :, 4, :, 0] = 1.96875 * 2.0 ** 8
        x[r, :, 5, :, 0] = rng.choice([-1.0, 1.0], (8, C)) * 2.0 ** -30
        x[r, :, 6, :, 0] = 2.0 ** -28
    w = layers(rng)
    w[:, :, :8] = 0
    w[:, :, :, :, :, :8] = 0
    for g in range(8):
        w[:, g, 5, 0, g, 0, 0] = 2.0 ** -8
        w[:, g, 5, 0, g, 2, 0] = 2.0 ** -8
        w[:, g, 5, 0, g, 6, 0] = 32.0
    return {"x": x.reshape(N, 128, 4 * C).astype(BF), "u": u.reshape(N, 128, 512), "v": d["v"], **wiring(rng), **weights(rng, w)}
def setup_inputs_late(rng):
    d = numbers_of(rng)
    c = (rng.permutation(N) % 2 * 2.0 - 1.0).astype(np.float32).astype(BF)
    x = d["x"].reshape(N, 8, 16, C, 4)
    x[:, :, :2] = c[:, None, None, None, None]
    u = blank(d)
    for h in range(0, 128, 16):
        for i in range(2): u[:, h + i, h + i, 0] = 1
    w = layers(rng)
    w[:, :, :, :, :, :2] = (w[:, :, :, :, :, :2].astype(np.float32) * 4).astype(BF)
    return {"x": x.reshape(N, 128, 4 * C), "u": u.reshape(N, 128, 512), "v": d["v"], **edges(rng), **weights(rng, w)}
def setup_inputs_ends(rng):
    d = numbers_of(rng)
    e = [0, STEP[0], STEP[1], STEP[0] ^ STEP[1]]
    e = e + [STEP[2] ^ i for i in e[:N - 4]]
    n = N // 4
    o = np.zeros(N, np.int64)
    o[np.array(e) ^ int(rng.integers(N))] = np.concatenate([np.full(n, 3), np.full(n, 2), rng.permutation(np.arange(2 * n) % 2)])
    x = np.zeros((N, 128, C, 4))
    u = blank(d).astype(np.float32)
    v = rng.choice([-1.0, 1.0], (N, 128, 512))
    w = np.zeros((N, 128, 4, 128, 4), np.float32)
    p = np.arange(128)
    for r in range(N):
        x[r] = (0.9 + 0.02 * rng.random((128, C, 4))) * 2.0 ** 30
        if o[r] == 0: x[r] *= -1
        if o[r] == 1: x[r] *= (1.0 - 2.0 * (np.arange(C) % 2))[None, :, None]
        if o[r] == 2: x[r] *= rng.choice([-1.0, 1.0], (128, C, 4))
        if o[r] == 3:
            x[r] = (1.0 + 0.125 * rng.integers(0, 8, (128, C, 4))) * 2.0 ** -30 * rng.choice([-1.0, 1.0], (1, C, 1))
            x[r, 0::8, :, 0] = 1.5 * 2.0 ** -29
        for i in range(2):
            h = rng.permutation(8)
            u[r, :, i::16] = np.where(h < 2, 0.0, h % 2 * 2.0 - 1.0)[None, :, None] * (2.0 ** -30 if o[r] == 3 else 2.0 ** 30)
        v[r] *= 2.0 ** 30 if o[r] % 2 == 0 else 2.0 ** -30
        for b in range(4): w[r, p, b, p, b] = [-0.25, -0.25, 2.0 ** -8, 256.0][o[r]]
    return {"x": x.astype(np.float32).reshape(N, 128, 4 * C).astype(BF), "u": u.reshape(N, 128, 512).astype(BF), "v": v.astype(np.float32).astype(BF), **edges(rng), **weights(rng, w.astype(BF))}
def setup_inputs_spread(rng):
    d = setup_inputs(rng)
    d["x"] = wide(rng, N, 128, 4 * C, cols=6)
    return d
def check_inputs(d):
    b = []
    for k in ("x", "u", "v"):
        a = np.abs(d[k].astype(np.float32))
        if not (np.isfinite(a).all() and ((a == 0) | (a >= 2.0 ** -30) & (a <= 2.0 ** 30)).all()): b.append("a value of " + k)
    none, least, most = [emit(mx_ref.quantize(np.full((128, 16), k, np.float32).astype(BF)))[1][0, 0] for k in (0.0, 2.0 ** -8, 2.0 ** 8)]
    for r in range(N):
        e, i = gentries(d["wl"][r]), np.arange(3 * C)
        if not ((e >= 0) & (e < 3 * C)).all(): b.append("an entry of wl")
        elif (e == i).any() or (np.take_along_axis(e, e, axis=1) != i).any(): b.append("wl: ports that aren't wired in pairs")
        if ((d["wc"][r] == 0x7F) | (d["wc"][r] == 0xFF)).any(): b.append("wc: a code that is no number")
        s = mx_ref.live(d["ws"][r])
        if ((s != none) & ((s < least) | (s > most))).any(): b.append("ws: a scale out of range")
    return b
def rewired(w, a, b):
    c, d = np.arange(C), w[:, :C]
    active = d < C
    same = a == np.take_along_axis(a, np.minimum(d, C - 1), axis=1)
    turn, cross, swap = active & same, active & ~same, ~active & b
    to = np.concatenate([np.where(turn | swap, c + C, c),
                         np.where(turn, c + 2 * C, np.where(cross, d + C, np.where(swap, c, c + C))),
                         np.where(turn, c, np.where(cross, d + 2 * C, c + 2 * C))], axis=1)
    new = np.zeros_like(to)
    np.put_along_axis(new, to, np.take_along_axis(to, w, axis=1), axis=1)
    return new
def reference(x, u, v, wl, wc, ws):
    qu = [mx_ref.quantize(u[r]) for r in range(N)]
    lay = [pk(wc[r], ws[r]) for r in range(N)]
    wire = [gentries(wl[r]).astype(np.int64) for r in range(N)]
    now = [x[r] for r in range(N)]
    for step in STEP:
        made = []
        for r in range(N):
            s = mx_ref.matmul(qu[r], mx_ref.quantize(now[r]))
            wire[r] = rewired(wire[r], s[0::16] > 0, s[1::16] > 0)
            one, two = gcols(now[r], wire[r][:, C:2 * C] % C), gcols(now[r], wire[r][:, 2 * C:] % C)
            z = mx_ref.quantize(((one.astype(np.float32) + two.astype(np.float32)) * np.float32(0.5)).astype(BF))
            made.append(mx_ref.quantize(tile([mx_ref.matmul(pick(lay[r], np.arange(128 * b, 128 * b + 128)), z) * np.float32(0.03125) for b in range(4)])))
        for r in range(N):
            p = r ^ step
            m = np.take_along_axis(wire[p], wire[r][:, :C], axis=1) % C
            now[r] = (now[r].astype(np.float32) + gcols(decode(made[p]).astype(BF), m).astype(np.float32)).astype(BF)
    y, ow = np.zeros((N, 128, C), np.float32), np.zeros((N, 8, 3 * C), np.float32)
    oc, osc = np.zeros((N, 128, 4 * C), np.uint8), np.zeros((N, 16, C), np.uint8)
    for r in range(N):
        q = mx_ref.quantize(now[r])
        y[r] = mx_ref.matmul(mx_ref.quantize(v[r]), q)
        ow[r] = wire[r]
        oc[r], osc[r] = emit(q)
    return {"y": y, "ow": ow, "oc": oc, "osc": osc}

@@ -1,0 +1,386 @@
+from concourse.mybir import dt, AluOpType, ActivationFunctionType as AF
+
+OP = AluOpType
+C = 384
+F = 3 * C
+K = 4194304.0
+ROUNDS = 3
+STEP = [1, 2, 3]
+RUNS = [(0, 192), (192, 384)]
+
+SCRATCH = {
+    "xt": ("sbuf", [128, 4 * C], "bfloat16"), "xh": ("sbuf", [128, 4 * C], "bfloat16"), "gz": ("sbuf", [128, 4 * C], "bfloat16"),
+    "zt": ("sbuf", [128, 4 * C], "bfloat16"), "hp": ("sbuf", [128, 4 * C], "bfloat16"), "hg": ("sbuf", [128, 4 * C], "bfloat16"),
+    "ut": ("sbuf", [128, 512], "bfloat16"), "vt": ("sbuf", [128, 512], "bfloat16"),
+    "ones": ("sbuf", [128, F], "bfloat16"), "eb": ("sbuf", [128, 516], "bfloat16"),
+    "uq": ("sbuf", [128, 128], "float8_e4m3fn_x4"), "us": ("sbuf", [128, 128], "uint8"),
+    "pq": ("sbuf", [128, 256], "float8_e4m3fn_x4"), "psc": ("sbuf", [128, 256], "uint8"),
+    "vq": ("sbuf", [128, 128], "float8_e4m3fn_x4"), "vs": ("sbuf", [128, 128], "uint8"),
+    "eq": ("sbuf", [128, 512], "float8_e4m3fn_x4"), "es": ("sbuf", [128, 512], "uint8"),
+    "wq": ("sbuf", [128, 512], "float8_e4m3fn_x4"), "wp": ("sbuf", [128, 512], "uint8"),
+    "xq": ("sbuf", [128, C], "float8_e4m3fn_x4"), "xs": ("sbuf", [128, C], "uint8"),
+    "zq": ("sbuf", [128, C], "float8_e4m3fn_x4"), "zs": ("sbuf", [128, C], "uint8"),
+    "wlt": ("sbuf", [128, 72], "int32"), "pi32": ("sbuf", [128, 1], "int32"), "p15i": ("sbuf", [128, 1], "int32"),
+    "p15": ("sbuf", [128, 1], "float32"), "p3": ("sbuf", [128, 1], "float32"), "last": ("sbuf", [128, 1], "float32"),
+    "inv": ("sbuf", [128, 1], "float32"), "inv3": ("sbuf", [128, 1], "float32"), "thp": ("sbuf", [128, 1], "float32"),
+    "c48": ("sbuf", [128, 24], "float32"), "c3": ("sbuf", [128, 24], "float32"),
+    "uoi": ("sbuf", [128, 16], "int32"), "uo": ("sbuf", [128, 16], "uint16"),
+    "jr": ("sbuf", [128, C], "float32"), "e0": ("sbuf", [128, C], "float32"), "e1": ("sbuf", [128, C], "float32"), "mask": ("sbuf", [128, C], "float32"),
+    "idr": ("sbuf", [128, F], "float32"), "qtab": ("sbuf", [128, F], "float32"), "acttab": ("sbuf", [128, F], "bfloat16"),
+    "pir": ("sbuf", [128, F], "float32"), "om0": ("sbuf", [128, F], "float32"), "om1": ("sbuf", [128, F], "float32"),
+    "ew": ("sbuf", [128, 2 * C], "float32"), "hrow": ("sbuf", [128, C], "float32"), "thr": ("sbuf", [128, C], "float32"),
+    "fr": ("sbuf", [128, C], "float32"), "fs": ("sbuf", [128, C], "float32"), "f72": ("sbuf", [128, 72], "float32"),
+    "sc": ("sbuf", [128, F], "float32"), "y12": ("sbuf", [128, 2 * C], "float32"), "sy": ("sbuf", [128, 2 * C], "float32"),
+    "mr": ("sbuf", [128, C], "float32"), "ms": ("sbuf", [128, C], "float32"), "ml": ("sbuf", [128, 24], "uint16"),
+    "l12": ("sbuf", [128, 48], "uint16"),
+    "q3": ("sbuf", [128, 72], "float32"), "k1": ("sbuf", [128, 72], "float32"), "k2": ("sbuf", [128, 72], "float32"), "kk": ("sbuf", [128, 72], "float32"),
+    "u0": ("sbuf", [128, 72], "float32"), "du": ("sbuf", [128, 72], "float32"), "w12": ("sbuf", [128, 48], "float32"),
+    "p0": ("sbuf", [128, 72], "float32"), "dp": ("sbuf", [128, 72], "float32"),
+    "mp": ("sbuf", [128, 72], "float32"), "sp": ("sbuf", [128, 72], "float32"), "p16": ("sbuf", [128, 72], "uint16"),
+    "mu": ("sbuf", [128, 72], "float32"), "su": ("sbuf", [128, 72], "float32"), "u16": ("sbuf", [128, 72], "uint16"),
+    "ai": ("sbuf", [128, 24], "int32"), "a3": ("sbuf", [128, 24], "float32"), "act": ("sbuf", [128, 24], "float32"),
+    "td": ("sbuf", [128, 24], "float32"), "ta": ("sbuf", [128, 24], "float32"), "tau": ("sbuf", [128, 24], "float32"),
+    "ad0": ("sbuf", [128, 24], "float32"), "ad": ("sbuf", [128, 24], "float32"), "x12": ("sbuf", [128, 48], "uint16"),
+    "a2m": ("sbuf", [128, 24], "float32"), "va": ("sbuf", [128, 24], "float32"), "vta": ("sbuf", [128, 24], "float32"), "ss": ("sbuf", [128, 24], "float32"),
+    "u10": ("sbuf", [128, 24], "float32"), "u12": ("sbuf", [128, 24], "float32"), "dst": ("sbuf", [128, 24], "uint16"),
+    "w16": ("sbuf", [128, 72], "uint16"), "fin": ("sbuf", [128, 72], "uint16"), "owr": ("sbuf", [128, F], "float32"), "yt": ("sbuf", [128, C], "float32"),
+    "ps": ("psum", [128, 4096], "float32"),
+}
+for _k in range(ROUNDS):
+    SCRATCH["dl%d" % _k] = ("sbuf", [128, 24], "uint16")
+    SCRATCH["la%d" % _k] = ("sbuf", [128, 24], "uint16")
+    for _n in ("h", "l"):
+        for _i in range(len(RUNS)):
+            SCRATCH["%sq%d%d" % (_n, _k, _i)] = ("sbuf", [128, RUNS[_i][1] - RUNS[_i][0]], "float8_e4m3fn_x4")
+            SCRATCH["%ss%d%d" % (_n, _k, _i)] = ("sbuf", [128, RUNS[_i][1] - RUNS[_i][0]], "uint8")
+SEMAPHORES = ["V", "A", "P", "G", "left"] + ["al%d" % k for k in range(ROUNDS)] + ["ah%d%d" % (k, i) for k in range(ROUNDS) for i in range(len(RUNS))] + ["d%d" % i for i in range(40)]
+
+
+def rank_program(g, core, T, topo):
+    rank = T.rank_of(core)
+    if rank is None:
+        return
+    QUEUE = {"V": g.vector, "A": g.scalar, "P": g.tensor, "G": g, "S": g.sync}
+    count = {}
+    seen = {}
+    book = {}
+
+    def wait(q, sem, val):
+        if seen.get((q, sem), 0) < val:
+            QUEUE[q].wait_ge(T.sem[sem], val)
+            seen[(q, sem)] = val
+
+    def region(r):
+        if len(r) == 3: return r[0], r[1], r[2], 1, 0
+        return r[0], r[1], r[2], r[3], r[1] % r[3]
+
+    def meets(a, b):
+        if a[0] >= b[1] or b[0] >= a[1]: return False
+        return not (a[2] == b[2] and a[3] != b[3])
+
+    def note(sem, val, reads, writes):
+        for r in reads:
+            n, lo, hi, st, ph = region(r)
+            book.setdefault(n, []).append((lo, hi, st, ph, sem, val, False))
+        for r in writes:
+            n, lo, hi, st, ph = region(r)
+            l = [e for e in book.get(n, []) if not (lo <= e[0] and e[1] <= hi and (st == 1 or (st, ph) == (e[2], e[3])))]
+            book[n] = l + [(lo, hi, st, ph, sem, val, True)]
+
+    def depend(q, reads, writes):
+        need = {}
+        for rs, w in ((reads, False), (writes, True)):
+            for r in rs:
+                n, lo, hi, st, ph = region(r)
+                for e in book.get(n, []):
+                    if (w or e[6]) and meets((lo, hi, st, ph), e): need[e[4]] = max(need.get(e[4], 0), e[5])
+        for sem in sorted(need): wait(q, sem, need[sem])
+
+    def op(q, reads, writes, call):
+        depend(q, reads, writes)
+        count[q] = count.get(q, 0) + 1
+        call(QUEUE[q]).then_inc(T.sem[q], 1)
+        note(q, count[q], reads, writes)
+
+    ndma = [0]
+
+    def dma(q, out, in_, reads, writes):
+        depend(q, reads, writes)
+        sem = "d%d" % ndma[0]
+        ndma[0] += 1
+        count[sem] = 16
+        QUEUE[q].dma_start(out, in_).then_inc(T.sem[sem], 16)
+        note(sem, 16, reads, writes)
+
+    def send(dst, out, in_, reads, sem):
+        depend("G", reads, [])
+        rid, pid, _ = topo.addr(dst)
+        m = topo.mask(core, dst)
+        count["left"] = count.get("left", 0) + len(topo.engines(core, dst))
+        g.remote_dma(out, in_, T.sem[sem], T.sem.left, pid, rid, m)
+
+    def ap(r):
+        return T[r[0]][:, r[1]:r[2]] if len(r) == 3 else T[r[0]][:, r[1]:r[2]:r[3]]
+
+    def apx(r):
+        return (ap(r[0]).indirect(ap(r[1])), [r[0], r[1]]) if not isinstance(r[0], str) else (ap(r), [r])
+
+    def tt(o, a, b, f):
+        x, rd = apx(a)
+        op("V", rd + [b], [o], lambda e: e.tensor_tensor(ap(o), x, ap(b), f))
+
+    def ts(o, a, s1, f1, s2=None, f2=None, q="V"):
+        x, rd = apx(a)
+        rd = list(rd)
+        if isinstance(s1, str):
+            rd.append((s1, 0, 1))
+            s1 = T[s1][:, 0:1]
+        if f2 is None: op(q, rd, [o], lambda e: e.tensor_scalar(ap(o), x, s1, None, f1))
+        else: op(q, rd, [o], lambda e: e.tensor_scalar(ap(o), x, s1, s2, f1, f2))
+
+    def cp(o, a):
+        x, rd = apx(a)
+        op("V", rd, [o], lambda e: e.tensor_copy(ap(o), x))
+
+    def ac(o, a, f=AF.Copy, scale=1.0):
+        x, rd = apx(a)
+        if scale == 1.0: op("A", rd, [o], lambda e: e.activation(ap(o), x, f))
+        else: op("A", rd, [o], lambda e: e.activation(ap(o), x, f, scale=scale))
+
+    def move(q, o, a):
+        (cp if q == "V" else ac)(o, a)
+
+    def scaled(q, o, a, s):
+        if q == "V": ts(o, a, s, OP.mult)
+        else: ac(o, a, scale=s)
+
+    def scan(o, a, f=OP.max):
+        op("V", [("mask", 0, C), a], [o], lambda e: e.tensor_tensor_scan(ap(o), T.mask[:, 0:C], ap(a), 0.0, OP.mult, f))
+
+    def quant(q, s, lo, hi, a):
+        op("V", [a], [(q, lo, hi), (s, lo, hi)], lambda e: e.quantize_mx(T[q][:, lo:hi], T[s][:, lo:hi], ap(a)))
+
+    def mm(bank, n, w, ws, wlo, x, xs, lo):
+        op("P", [(w, wlo, wlo + 128), (ws, wlo, wlo + 128), (x, lo, lo + n), (xs, lo, lo + n)], [("ps", 512 * bank, 512 * bank + 512)],
+           lambda e: e.matmul_mx(T.ps[:, 512 * bank:512 * bank + n], T[w][:, wlo:wlo + 128], T[ws][:, wlo:wlo + 128], T[x][:, lo:lo + n], T[xs][:, lo:lo + n], True, True))
+
+    def psum(bank, n):
+        return ("ps", 512 * bank, 512 * bank + n)
+
+    def ends(b, i=0):
+        return (b, C * i + 15, C * i + C, 16)
+
+    def ports(o, s):
+        ts(o, s, "inv", OP.mult, -1.0, OP.add)
+
+    def agents(o, s):
+        ts(o, s, "inv3", OP.mult, -2.0 / 3.0, OP.add)
+
+    dma("A", T.wlt[:, 0:72], T.wl[:, :], [], [("wlt", 0, 72)])
+    dma("S", T.ut[:, 0:512], T.u[:, :], [], [("ut", 0, 512)])
+    for i, (lo, hi) in enumerate(RUNS): dma("AS"[i], T.xt[:, 4 * lo:4 * hi], T.x[:, 4 * lo:4 * hi], [], [("xt", 4 * lo, 4 * hi)])
+    dma("S", T.wq[:, 0:512].bitcast(dt.uint8), T.wc[:, :], [], [("wq", 0, 512)])
+    dma("S", T.wp[:, 0:512], T.ws[:, :], [], [("wp", 0, 512)])
+    dma("S", T.vt[:, 0:512], T.v[:, :], [], [("vt", 0, 512)])
+
+    def iota(r, pattern, base, mult, flag):
+        op("G", [], [r], lambda e: e.iota(ap(r), pattern, base, mult, allow_small_or_imprecise_dtypes=True) if flag else e.iota(ap(r), pattern, base, mult))
+    iota(("pi32", 0, 1), [[0, 1]], 0, 1, False)
+    iota(("c48", 0, 24), [[48, 24]], 0, 0, True)
+    iota(("uoi", 0, 16), [[1, 2], [16, 8]], 0, 0, False)
+    iota(("jr", 0, C), [[0, 24], [1, 16]], 0, 0, True)
+    op("V", [], [("ones", 0, F)], lambda e: e.memset(T.ones[:, 0:F], 1.0))
+    op("V", [("ones", 0, F)], [("idr", 0, F)], lambda e: e.tensor_tensor_scan(T.idr[:, 0:F], T.ones[:, 0:F], T.ones[:, 0:F], 0.0, OP.mult, OP.add))
+    op("G", [("ones", 0, 516)], [("eb", 0, 516)], lambda e: e.affine_select(T.eb[:, 0:516], T.ones[:, 0:516], [[-1, 516]], OP.is_equal, 0.0, 3, 4))
+    for k in range(3): iota(("qtab", k, F, 3), [[1, C]], C * k, 0, True)
+    ts(("p15i", 0, 1), ("pi32", 0, 1), 15, OP.bitwise_and)
+    cp(("uo", 0, 16), ("uoi", 0, 16))
+    cp(("p15", 0, 1), ("p15i", 0, 1))
+    ts(("p3", 0, 1), ("p15", 0, 1), 3.0, OP.mult)
+    ts(("last", 0, 1), ("p15", 0, 1), 15.0, OP.is_equal)
+    ts(("c3", 0, 24), ("c48", 0, 24), "p3", OP.add)
+    ts(("inv", 0, 1), ("last", 0, 1), 1.0 - 1.0 / K, OP.mult, 1.0 / K, OP.add)
+    ts(("thp", 0, 1), ("last", 0, 1), 1.0 - K, OP.mult, K, OP.add)
+    ts(("inv3", 0, 1), ("inv", 0, 1), 1.0 / 3.0, OP.mult)
+    cp(("p0", 0, 24), ("c3", 0, 24))
+    op("V", [], [("acttab", 0, F)], lambda e: e.memset(T.acttab[:, 0:F], -1e29))
+    op("V", [], [("acttab", 0, F, 3)], lambda e: e.memset(T.acttab[:, 0:F:3], 0.0))
+
+    w72 = ("wlt", 0, 72)
+    ts(("k1", 0, 72), w72, 384.0, OP.is_ge, -1151.0, OP.mult)
+    ts(("k2", 0, 72), w72, 768.0, OP.is_ge, -1151.0, OP.mult)
+    ts(("q3", 0, 72), w72, 3.0, OP.mult)
+    tt(("kk", 0, 72), ("k1", 0, 72), ("k2", 0, 72), OP.add)
+    tt(("k1", 0, 72), ("q3", 0, 72), ("kk", 0, 72), OP.add)
+    cp(("w16", 0, 72), ("k1", 0, 72))
+    cp(("u0", 0, 24), ("k1", 0, 24))
+    cp(("w12", 0, 48), ("k1", 24, 72))
+    move("A", ("om0", 1, F, 3), (("idr", 0, F), ("w16", 24, 48)))
+    move("A", ("om0", 2, F, 3), (("idr", 0, F), ("w16", 48, 72)))
+    move("V", ("om0", 0, F, 3), (("idr", 0, F), ("w16", 0, 24)))
+
+    W0, W1, W2 = ("u0", 0, 24), ("w12", 0, 24), ("w12", 24, 48)
+
+    def ready1(om, lst, loff, meanwhile=None):
+        z = lambda n: (n, 0, 24)
+        ts(z("ai"), W0, 1.0 / 3.0, OP.mult, -1.0 / 3.0, OP.add)
+        tt(z("td"), W0, z("c3"), OP.subtract)
+        tt(z("ad0"), W2, W1, OP.subtract)
+        ts(z("a3"), z("ai"), 3.0, OP.mult)
+        tt(z("act"), W0, z("a3"), OP.is_equal)
+        move("A", ("thr", 0, C), (("acttab", 0, F), (lst, loff, loff + 24)))
+        tt(z("ta"), z("td"), z("act"), OP.mult)
+        tt(z("tau"), z("ta"), z("c3"), OP.add)
+        ts(z("va"), z("act"), -1152.0, OP.mult, 1152.0, OP.add)
+        ts(("x12", 0, 24), z("tau"), 1.0, OP.add)
+        ts(("x12", 24, 48), z("tau"), 2.0, OP.add)
+        move("A", ("y12", 0, C), ((om, 0, F), ("x12", 0, 24)))
+        move("A", ("y12", C, 2 * C), ((om, 0, F), ("x12", 24, 48)))
+        if meanwhile: meanwhile()
+        tt(z("vta"), z("va"), z("tau"), OP.add)
+        ts(z("dst"), z("vta"), 1.0 / 3.0, OP.mult)
+        ts(z("a2m"), z("act"), 2.0, OP.mult, -1.0, OP.add)
+        tt(z("ad"), z("ad0"), z("act"), OP.mult)
+        ts(("p0", 24, 48), z("tau"), 1.0, OP.add)
+        ts(("p0", 48, 72), z("tau"), 2.0, OP.add)
+        tt(z("ss"), z("a2m"), z("ta"), OP.add)
+        tt(("dp", 24, 48), z("a2m"), z("ta"), OP.subtract)
+        tt(z("u10"), W1, z("ad"), OP.add)
+        tt(z("u12"), W2, z("ad"), OP.subtract)
+        ts(("dp", 48, 72), z("ss"), -1.0, OP.mult, -1.0, OP.add)
+        tt(("du", 0, 24), z("u10"), W0, OP.subtract)
+
+    def ready2():
+        scan(("sy", 0, C), ("y12", 0, C))
+        scan(("sy", C, 2 * C), ("y12", C, 2 * C))
+        ports(("u0", 24, 48), ends("sy", 0))
+        ports(("u0", 48, 72), ends("sy", 1))
+        tt(("du", 24, 48), W0, ("u0", 24, 48), OP.subtract)
+        tt(("du", 48, 72), ("u12", 0, 24), ("u0", 48, 72), OP.subtract)
+
+    def quantx(i):
+        lo, hi = RUNS[i]
+        quant("xq", "xs", lo, hi, ("xt", 4 * lo, 4 * hi))
+
+    def scores(i):
+        lo, hi = RUNS[i]
+        mm(4 - 4 * i, hi - lo, "pq", "psc", 0, "xq", "xs", lo)
+        mm(5 - 4 * i, hi - lo, "pq", "psc", 128, "xq", "xs", lo)
+
+    def signs(i):
+        lo, hi = RUNS[i]
+        n = hi - lo
+        ts(("ew", lo, hi), psum(4 - 4 * i, n), 0.0, OP.is_gt)
+        ac(("ew", C + lo, C + hi), psum(5 - 4 * i, n), AF.Sign)
+        tt(("hrow", lo, hi), psum(4 - 4 * i, n), ("thr", lo, hi), OP.is_gt)
+
+    def halves(i):
+        lo, hi = RUNS[i]
+        for b in range(4): ac(("xh", C * b + lo, C * b + hi), ("xt", 4 * lo + b, 4 * hi, 4), scale=0.5)
+
+    def first():
+        ts(("e0", 0, C), ("jr", 0, C), "p15", OP.subtract)
+        ts(("e1", 0, C), ("e0", 0, C), 1.0, OP.is_equal, K - 1.0, OP.mult)
+        ts(("jr", 0, C), ("e0", 0, C), 0.0, OP.is_equal, -1.0, OP.mult)
+        quant("uq", "us", 0, 128, ("ut", 0, 512))
+        op("A", [("us", 0, 128), ("uo", 0, 16)], [("psc", 0, 256)], lambda e: e.activation(T.psc[:, 0:256], T.us[:, 0:128].indirect(T.uo[:, 0:16]), AF.Copy))
+        op("V", [("uq", 0, 128), ("uo", 0, 16)], [("pq", 0, 256)], lambda e: e.tensor_copy(T.pq[:, 0:256].bitcast(dt.uint32), T.uq[:, 0:128].bitcast(dt.uint32).indirect(T.uo[:, 0:16])))
+        tt(("e0", 0, C), ("e1", 0, C), ("jr", 0, C), OP.add)
+        quantx(0)
+        ts(("mask", 0, C), ("e0", 0, C), 1.0, OP.add)
+        quantx(1)
+        scores(0)
+        scores(1)
+
+    ready1("om0", "w16", 0, first)
+    halves(0)
+    ready2()
+    signs(0)
+    signs(1)
+    halves(1)
+
+    for k in range(ROUNDS):
+        old, new = ("om0", "om1") if k % 2 == 0 else ("om1", "om0")
+        peer = T.cores[rank ^ STEP[k]]
+        dl, la, last = "dl%d" % k, "la%d" % k, k == ROUNDS - 1
+        tt(("fr", 0, C), (("ew", 0, 2 * C), ("dst", 0, 24)), ("hrow", 0, C), OP.is_equal)
+        scan(("fs", 0, C), ("fr", 0, C), OP.add)
+        z = lambda n: (n, 0, 72)
+        f = ("mp", 0, 24)
+        ts(f, ends("fs"), "thp", OP.is_ge)
+        for j in (1, 2): tt(("mp", 24 * j, 24 * j + 24), ("dp", 24 * j, 24 * j + 24), f, OP.mult)
+        tt(z("sp"), z("mp"), z("p0"), OP.add)
+        cp(z("p16"), z("sp"))
+        move("A", ("pir", 1, F, 3), (("idr", 0, F), ("p16", 24, 48)))
+        move("A", ("pir", 2, F, 3), (("idr", 0, F), ("p16", 48, 72)))
+        for j in range(3): tt(("mu", 24 * j, 24 * j + 24), ("du", 24 * j, 24 * j + 24), f, OP.mult)
+        tt(z("su"), z("mu"), z("u0"), OP.add)
+        cp(z("u16"), z("su"))
+        move("V", ("pir", 0, F, 3), (("idr", 0, F), ("p16", 0, 24)))
+        for q, j in (("V", 1), ("A", 2), ("A", 0)): move(q, (new, j, F, 3), (("pir", 0, F), ("u16", 24 * j, 24 * j + 24)))
+        scan(("sc", C, 2 * C), (new, 1, F, 3))
+        agents(("l12", 0, 24), ends("sc", 1))
+        scan(("sc", 2 * C, 3 * C), (new, 2, F, 3))
+        agents(("l12", 24, 48), ends("sc", 2))
+        scan(("sc", 0, C), (new, 0, F, 3))
+        ports((dl, 0, 24), ends("sc", 0))
+        send(peer, T[la][:, 0:24], T[dl][:, 0:24], [(dl, 0, 24)], "al%d" % k)
+        note("al%d" % k, len(topo.engines(core, peer)), [], [(la, 0, 24)])
+        for i, (lo, hi) in enumerate(RUNS):
+            for b in range(4): move("A", ("gz", C * b + lo, C * b + hi), (("xh", C * b, C * b + C), ("l12", lo // 16, hi // 16)))
+        for i, (lo, hi) in enumerate(RUNS):
+            for b in range(4): tt(("zt", 4 * lo + b, 4 * hi, 4), (("xh", C * b, C * b + C), ("l12", 24 + lo // 16, 24 + hi // 16)), ("gz", C * b + lo, C * b + hi), OP.add)
+            quant("zq", "zs", lo, hi, ("zt", 4 * lo, 4 * hi))
+            for b in range(4): mm(4 * i + b, hi - lo, "wq", "wp", 128 * b, "zq", "zs", lo)
+        def places():
+            move("A", ("mr", 0, C), ((new, 0, F), (la, 0, 24)))
+            scan(("ms", 0, C), ("mr", 0, C))
+            agents(("ml", 0, 24), ends("ms"))
+        for i, (lo, hi) in enumerate(RUNS):
+            if i == 1 and k > 0: places()
+            for q, b in (("V", 0), ("A", 1), ("V", 2), ("A", 3)): scaled(q, ("hp", C * b + lo, C * b + hi), psum(4 * i + b, hi - lo), 0.03125)
+        if k == 0: places()
+        for i, (lo, hi) in enumerate(RUNS):
+            hq, hs, lq, ls, n = "hq%d%d" % (k, i), "hs%d%d" % (k, i), "lq%d%d" % (k, i), "ls%d%d" % (k, i), hi - lo
+            for q, b in (("V", 0), ("A", 1), ("V", 2), ("A", 3)):
+                move(q, ("hg", 4 * lo + b, 4 * hi, 4), (("hp", C * b, C * b + C), ("ml", lo // 16, hi // 16)))
+            quant(hq, hs, 0, n, ("hg", 4 * lo, 4 * hi))
+            send(peer, T[lq][:, 0:n].bitcast(dt.uint8), T[hq][:, 0:n].bitcast(dt.uint8), [(hq, 0, n)], "ah%d%d" % (k, i))
+            send(peer, T[ls][:, 0:n], T[hs][:, 0:n], [(hs, 0, n)], "ah%d%d" % (k, i))
+            note("ah%d%d" % (k, i), 2 * len(topo.engines(core, peer)), [], [(lq, 0, n), (ls, 0, n)])
+        if k == 0:
+            for b in range(4): quant("eq", "es", 128 * b, 128 * b + 128, ("eb", 3 - b, 515 - b))
+        if k == 1: quant("vq", "vs", 0, 128, ("vt", 0, 512))
+        if not last:
+            ports(W0, ends("sc", 0))
+            ports(W1, ends("sc", 1))
+            ports(W2, ends("sc", 2))
+            ready1(new, dl, 0)
+            ready2()
+        else:
+            for j in range(3): ports(("fin", 24 * j, 24 * j + 24), ends("sc", j))
+            move("A", ("owr", 0, F), (("qtab", 0, F), ("fin", 0, 72)))
+            for j in range(8): dma("S", T.ow[j:j + 1, :], T.owr[16 * j:16 * j + 1, 0:F], [("owr", 0, F)], [])
+        for i, (lo, hi) in enumerate(RUNS):
+            for b in range(4): mm(4 - 4 * i + b, hi - lo, "eq", "es", 128 * b, "lq%d%d" % (k, i), "ls%d%d" % (k, i), 0)
+        for i, (lo, hi) in enumerate(RUNS):
+            for b in range(4):
+                x = ("xt", 4 * lo + b, 4 * hi, 4)
+                tt(x, psum(4 - 4 * i + b, hi - lo), x, OP.add)
+            quantx(i)
+            if not last:
+                scores(i)
+                if i == 1:
+                    halves(0)
+                    signs(0)
+                    signs(1)
+                    halves(1)
+            else:
+                n = hi - lo
+                mm(4 - 4 * i, n, "vq", "vs", 0, "xq", "xs", lo)
+                dma("S", T.oc[:, 4 * lo:4 * hi], T.xq[:, lo:hi].bitcast(dt.uint8), [("xq", lo, hi)], [])
+                for j in range(4): dma("A" if j % 2 else "S", T.osc[4 * j:4 * j + 4, lo:hi], T.xs[32 * j:32 * j + 4, lo:hi], [("xs", lo, hi)], [])
+                ac(("yt", lo, hi), psum(4 - 4 * i, n))
+                dma("A", T.y[:, lo:hi], T.yt[:, lo:hi], [("yt", lo, hi)], [])
+    for sem in ("V", "A", "P", "G", "left"): wait("G", sem, count[sem])
+    for j in range(ndma[0]): wait("G", "d%d" % j, 16)

@@ -7,6 +7,8 @@ K = 4194304.0
 ROUNDS = 3
 STEP = [1, 2, 3]
 RUNS = [(0, 192), (192, 384)]
+EXCHANGE = [RUNS, RUNS, [(0, 128), (128, 256), (256, 384)]]
+ZRUNS = [(0, 256), (256, 384)]
 
 SCRATCH = {
     "xt": ("sbuf", [128, 4 * C], "bfloat16"), "xh": ("sbuf", [128, 4 * C], "bfloat16"), "gz": ("sbuf", [128, 4 * C], "bfloat16"),
@@ -16,7 +18,8 @@ SCRATCH = {
     "uq": ("sbuf", [128, 128], "float8_e4m3fn_x4"), "us": ("sbuf", [128, 128], "uint8"),
     "pq": ("sbuf", [128, 256], "float8_e4m3fn_x4"), "psc": ("sbuf", [128, 256], "uint8"),
     "vq": ("sbuf", [128, 128], "float8_e4m3fn_x4"), "vs": ("sbuf", [128, 128], "uint8"),
-    "eq": ("sbuf", [128, 512], "float8_e4m3fn_x4"), "es": ("sbuf", [128, 512], "uint8"),
+    "em": ("sbuf", [128, 256], "float8_e4m3fn_x4"), "ems": ("sbuf", [128, 256], "uint8"), "el": ("sbuf", [128, 256], "float8_e4m3fn_x4"), "els": ("sbuf", [128, 256], "uint8"),
+    "sg": ("sbuf", [128, 192], "float32"),
     "wq": ("sbuf", [128, 512], "float8_e4m3fn_x4"), "wp": ("sbuf", [128, 512], "uint8"),
     "xq": ("sbuf", [128, C], "float8_e4m3fn_x4"), "xs": ("sbuf", [128, C], "uint8"),
     "zq": ("sbuf", [128, C], "float8_e4m3fn_x4"), "zs": ("sbuf", [128, C], "uint8"),
@@ -25,11 +28,12 @@ SCRATCH = {
     "inv": ("sbuf", [128, 1], "float32"), "inv3": ("sbuf", [128, 1], "float32"), "thp": ("sbuf", [128, 1], "float32"),
     "c48": ("sbuf", [128, 24], "float32"), "c3": ("sbuf", [128, 24], "float32"),
     "uoi": ("sbuf", [128, 16], "int32"), "uo": ("sbuf", [128, 16], "uint16"),
-    "jr": ("sbuf", [128, C], "float32"), "e0": ("sbuf", [128, C], "float32"), "e1": ("sbuf", [128, C], "float32"), "mask": ("sbuf", [128, C], "float32"),
+    "np15": ("sbuf", [128, 1], "float32"), "np16": ("sbuf", [128, 1], "float32"),
+    "jr": ("sbuf", [128, 96], "float32"), "e0": ("sbuf", [128, 96], "float32"), "e1": ("sbuf", [128, 96], "float32"), "e2": ("sbuf", [128, 96], "float32"), "e3": ("sbuf", [128, 96], "float32"), "mask": ("sbuf", [128, C], "float32"),
     "idr": ("sbuf", [128, F], "float32"), "qtab": ("sbuf", [128, F], "float32"), "acttab": ("sbuf", [128, F], "bfloat16"),
     "pir": ("sbuf", [128, F], "float32"), "om0": ("sbuf", [128, F], "float32"), "om1": ("sbuf", [128, F], "float32"),
     "ew": ("sbuf", [128, 2 * C], "float32"), "hrow": ("sbuf", [128, C], "float32"), "thr": ("sbuf", [128, C], "float32"),
-    "fr": ("sbuf", [128, C], "float32"), "fs": ("sbuf", [128, C], "float32"), "f72": ("sbuf", [128, 72], "float32"),
+    "fr": ("sbuf", [128, C], "float32"), "fs": ("sbuf", [128, C], "float32"),
     "sc": ("sbuf", [128, F], "float32"), "y12": ("sbuf", [128, 2 * C], "float32"), "sy": ("sbuf", [128, 2 * C], "float32"),
     "mr": ("sbuf", [128, C], "float32"), "ms": ("sbuf", [128, C], "float32"), "ml": ("sbuf", [128, 24], "uint16"),
     "l12": ("sbuf", [128, 48], "uint16"),
@@ -50,10 +54,9 @@ for _k in range(ROUNDS):
     SCRATCH["dl%d" % _k] = ("sbuf", [128, 24], "uint16")
     SCRATCH["la%d" % _k] = ("sbuf", [128, 24], "uint16")
     for _n in ("h", "l"):
-        for _i in range(len(RUNS)):
-            SCRATCH["%sq%d%d" % (_n, _k, _i)] = ("sbuf", [128, RUNS[_i][1] - RUNS[_i][0]], "float8_e4m3fn_x4")
-            SCRATCH["%ss%d%d" % (_n, _k, _i)] = ("sbuf", [128, RUNS[_i][1] - RUNS[_i][0]], "uint8")
-SEMAPHORES = ["V", "A", "P", "G", "left"] + ["al%d" % k for k in range(ROUNDS)] + ["ah%d%d" % (k, i) for k in range(ROUNDS) for i in range(len(RUNS))] + ["d%d" % i for i in range(40)]
+        SCRATCH["%sq%d" % (_n, _k)] = ("sbuf", [128, C], "float8_e4m3fn_x4")
+        SCRATCH["%ss%d" % (_n, _k)] = ("sbuf", [128, C], "uint8")
+SEMAPHORES = ["V", "A", "P", "G", "left", "ae"] + ["al%d" % k for k in range(ROUNDS)] + ["ah%d%d" % (k, i) for k in range(ROUNDS) for i in range(len(EXCHANGE[k]))] + ["d%d" % i for i in range(40)]
 
 
 def rank_program(g, core, T, topo):
@@ -142,10 +145,16 @@ def rank_program(g, core, T, topo):
         x, rd = apx(a)
         op("V", rd, [o], lambda e: e.tensor_copy(ap(o), x))
 
-    def ac(o, a, f=AF.Copy, scale=1.0):
+    def ac(o, a, f=AF.Copy, scale=1.0, bias=0.0):
         x, rd = apx(a)
-        if scale == 1.0: op("A", rd, [o], lambda e: e.activation(ap(o), x, f))
-        else: op("A", rd, [o], lambda e: e.activation(ap(o), x, f, scale=scale))
+        rd = list(rd)
+        arg = {}
+        for n, s, plain in (("bias", bias, 0.0), ("scale", scale, 1.0)):
+            if isinstance(s, str):
+                rd.append((s, 0, 1))
+                arg[n] = T[s][:, 0:1]
+            elif s != plain: arg[n] = s
+        op("A", rd, [o], lambda e: e.activation(ap(o), x, f, **arg))
 
     def move(q, o, a):
         (cp if q == "V" else ac)(o, a)
@@ -173,6 +182,9 @@ def rank_program(g, core, T, topo):
     def ports(o, s):
         ts(o, s, "inv", OP.mult, -1.0, OP.add)
 
+    def wraps(o, s):
+        ac(o, s, AF.Identity, scale="inv", bias=-1.0)
+
     def agents(o, s):
         ts(o, s, "inv3", OP.mult, -2.0 / 3.0, OP.add)
 
@@ -188,14 +200,21 @@ def rank_program(g, core, T, topo):
     iota(("pi32", 0, 1), [[0, 1]], 0, 1, False)
     iota(("c48", 0, 24), [[48, 24]], 0, 0, True)
     iota(("uoi", 0, 16), [[1, 2], [16, 8]], 0, 0, False)
-    iota(("jr", 0, C), [[0, 24], [1, 16]], 0, 0, True)
+    iota(("jr", 0, 96), [[0, 6], [1, 16]], 0, 0, True)
+    side = 0 if rank < (rank ^ STEP[0]) else 1
     op("V", [], [("ones", 0, F)], lambda e: e.memset(T.ones[:, 0:F], 1.0))
+    for j in range(3): ac(("acttab", j, F, 3), ("ones", 0, C), scale=-1e29 if j else 0.0)
+    ts(("p15i", 0, 1), ("pi32", 0, 1), 15, OP.bitwise_and)
+    cp(("p15", 0, 1), ("p15i", 0, 1))
+    ts(("np15", 0, 1), ("p15", 0, 1), -1.0, OP.mult)
+    ts(("np16", 0, 1), ("p15", 0, 1), -1.0, OP.mult, -1.0, OP.add)
+    ac(("e0", 0, 96), ("jr", 0, 96), AF.Sign, bias="np15")
+    ac(("e1", 0, 96), ("jr", 0, 96), AF.Abs, bias="np16")
+    ac(("e2", 0, 96), ("e0", 0, 96), AF.Abs)
+    ac(("e3", 0, 96), ("e1", 0, 96), AF.Relu, scale=-K, bias=K)
     op("V", [("ones", 0, F)], [("idr", 0, F)], lambda e: e.tensor_tensor_scan(T.idr[:, 0:F], T.ones[:, 0:F], T.ones[:, 0:F], 0.0, OP.mult, OP.add))
     op("G", [("ones", 0, 516)], [("eb", 0, 516)], lambda e: e.affine_select(T.eb[:, 0:516], T.ones[:, 0:516], [[-1, 516]], OP.is_equal, 0.0, 3, 4))
-    for k in range(3): iota(("qtab", k, F, 3), [[1, C]], C * k, 0, True)
-    ts(("p15i", 0, 1), ("pi32", 0, 1), 15, OP.bitwise_and)
     cp(("uo", 0, 16), ("uoi", 0, 16))
-    cp(("p15", 0, 1), ("p15i", 0, 1))
     ts(("p3", 0, 1), ("p15", 0, 1), 3.0, OP.mult)
     ts(("last", 0, 1), ("p15", 0, 1), 15.0, OP.is_equal)
     ts(("c3", 0, 24), ("c48", 0, 24), "p3", OP.add)
@@ -203,8 +222,9 @@ def rank_program(g, core, T, topo):
     ts(("thp", 0, 1), ("last", 0, 1), 1.0 - K, OP.mult, K, OP.add)
     ts(("inv3", 0, 1), ("inv", 0, 1), 1.0 / 3.0, OP.mult)
     cp(("p0", 0, 24), ("c3", 0, 24))
-    op("V", [], [("acttab", 0, F)], lambda e: e.memset(T.acttab[:, 0:F], -1e29))
-    op("V", [], [("acttab", 0, F, 3)], lambda e: e.memset(T.acttab[:, 0:F:3], 0.0))
+    tt(("mask", 0, 96), ("e2", 0, 96), ("e3", 0, 96), OP.max)
+    ac(("mask", 96, 192), ("mask", 0, 96))
+    ac(("mask", 192, C), ("mask", 0, 192))
 
     w72 = ("wlt", 0, 72)
     ts(("k1", 0, 72), w72, 384.0, OP.is_ge, -1151.0, OP.mult)
@@ -213,53 +233,47 @@ def rank_program(g, core, T, topo):
     tt(("kk", 0, 72), ("k1", 0, 72), ("k2", 0, 72), OP.add)
     tt(("k1", 0, 72), ("q3", 0, 72), ("kk", 0, 72), OP.add)
     cp(("w16", 0, 72), ("k1", 0, 72))
-    cp(("u0", 0, 24), ("k1", 0, 24))
-    cp(("w12", 0, 48), ("k1", 24, 72))
     move("A", ("om0", 1, F, 3), (("idr", 0, F), ("w16", 24, 48)))
     move("A", ("om0", 2, F, 3), (("idr", 0, F), ("w16", 48, 72)))
     move("V", ("om0", 0, F, 3), (("idr", 0, F), ("w16", 0, 24)))
 
     W0, W1, W2 = ("u0", 0, 24), ("w12", 0, 24), ("w12", 24, 48)
 
-    def ready1(om, lst, loff, meanwhile=None):
+    def ready1(om, lst, loff, W0, W1, W2, meanwhile=None):
         z = lambda n: (n, 0, 24)
         ts(z("ai"), W0, 1.0 / 3.0, OP.mult, -1.0 / 3.0, OP.add)
         tt(z("td"), W0, z("c3"), OP.subtract)
         tt(z("ad0"), W2, W1, OP.subtract)
         ts(z("a3"), z("ai"), 3.0, OP.mult)
         tt(z("act"), W0, z("a3"), OP.is_equal)
-        move("A", ("thr", 0, C), (("acttab", 0, F), (lst, loff, loff + 24)))
+        if not meanwhile: move("A", ("thr", 0, C), (("acttab", 0, F), (lst, loff, loff + 24)))
         tt(z("ta"), z("td"), z("act"), OP.mult)
         tt(z("tau"), z("ta"), z("c3"), OP.add)
-        ts(z("va"), z("act"), -1152.0, OP.mult, 1152.0, OP.add)
-        ts(("x12", 0, 24), z("tau"), 1.0, OP.add)
-        ts(("x12", 24, 48), z("tau"), 2.0, OP.add)
-        move("A", ("y12", 0, C), ((om, 0, F), ("x12", 0, 24)))
-        move("A", ("y12", C, 2 * C), ((om, 0, F), ("x12", 24, 48)))
-        if meanwhile: meanwhile()
-        tt(z("vta"), z("va"), z("tau"), OP.add)
-        ts(z("dst"), z("vta"), 1.0 / 3.0, OP.mult)
-        ts(z("a2m"), z("act"), 2.0, OP.mult, -1.0, OP.add)
-        tt(z("ad"), z("ad0"), z("act"), OP.mult)
         ts(("p0", 24, 48), z("tau"), 1.0, OP.add)
         ts(("p0", 48, 72), z("tau"), 2.0, OP.add)
+        cp(("x12", 0, 48), ("p0", 24, 72))
+        if meanwhile: meanwhile()
+        ac(z("va"), z("act"), AF.Identity, scale=-1152.0, bias=1152.0)
+        ac(z("a2m"), z("act"), AF.Identity, scale=2.0, bias=-1.0)
+        move("A", ("y12", 0, C), ((om, 0, F), ("x12", 0, 24)))
+        move("A", ("y12", C, 2 * C), ((om, 0, F), ("x12", 24, 48)))
+        if meanwhile: move("A", ("thr", 0, C), (("acttab", 0, F), (lst, loff, loff + 24)))
+        tt(z("ad"), z("ad0"), z("act"), OP.mult)
+        tt(z("vta"), z("va"), z("tau"), OP.add)
         tt(z("ss"), z("a2m"), z("ta"), OP.add)
+        ts(z("dst"), z("vta"), 1.0 / 3.0, OP.mult)
         tt(("dp", 24, 48), z("a2m"), z("ta"), OP.subtract)
+        ac(("dp", 48, 72), z("ss"), AF.Identity, scale=-1.0, bias=-1.0)
         tt(z("u10"), W1, z("ad"), OP.add)
         tt(z("u12"), W2, z("ad"), OP.subtract)
-        ts(("dp", 48, 72), z("ss"), -1.0, OP.mult, -1.0, OP.add)
         tt(("du", 0, 24), z("u10"), W0, OP.subtract)
 
     def ready2():
         scan(("sy", 0, C), ("y12", 0, C))
         scan(("sy", C, 2 * C), ("y12", C, 2 * C))
-        ports(("u0", 24, 48), ends("sy", 0))
-        ports(("u0", 48, 72), ends("sy", 1))
-        tt(("du", 24, 48), W0, ("u0", 24, 48), OP.subtract)
-        tt(("du", 48, 72), ("u12", 0, 24), ("u0", 48, 72), OP.subtract)
+        for j in range(2): wraps(("u0", 24 + 24 * j, 48 + 24 * j), ends("sy", j))
 
-    def quantx(i):
-        lo, hi = RUNS[i]
+    def quantx(lo, hi):
         quant("xq", "xs", lo, hi, ("xt", 4 * lo, 4 * hi))
 
     def scores(i):
@@ -267,10 +281,13 @@ def rank_program(g, core, T, topo):
         mm(4 - 4 * i, hi - lo, "pq", "psc", 0, "xq", "xs", lo)
         mm(5 - 4 * i, hi - lo, "pq", "psc", 128, "xq", "xs", lo)
 
-    def signs(i):
+    def signs(i, q="V"):
         lo, hi = RUNS[i]
         n = hi - lo
-        ts(("ew", lo, hi), psum(4 - 4 * i, n), 0.0, OP.is_gt)
+        if q == "V": ts(("ew", lo, hi), psum(4 - 4 * i, n), 0.0, OP.is_gt)
+        else:
+            op("A", [], [("sg", 0, n), psum(4 - 4 * i, n)], lambda e: e.activation(T.sg[:, 0:n], ap(psum(4 - 4 * i, n)), AF.Sign))
+            ac(("ew", lo, hi), ("sg", 0, n), AF.Relu)
         ac(("ew", C + lo, C + hi), psum(5 - 4 * i, n), AF.Sign)
         tt(("hrow", lo, hi), psum(4 - 4 * i, n), ("thr", lo, hi), OP.is_gt)
 
@@ -279,24 +296,27 @@ def rank_program(g, core, T, topo):
         for b in range(4): ac(("xh", C * b + lo, C * b + hi), ("xt", 4 * lo + b, 4 * hi, 4), scale=0.5)
 
     def first():
-        ts(("e0", 0, C), ("jr", 0, C), "p15", OP.subtract)
-        ts(("e1", 0, C), ("e0", 0, C), 1.0, OP.is_equal, K - 1.0, OP.mult)
-        ts(("jr", 0, C), ("e0", 0, C), 0.0, OP.is_equal, -1.0, OP.mult)
         quant("uq", "us", 0, 128, ("ut", 0, 512))
         op("A", [("us", 0, 128), ("uo", 0, 16)], [("psc", 0, 256)], lambda e: e.activation(T.psc[:, 0:256], T.us[:, 0:128].indirect(T.uo[:, 0:16]), AF.Copy))
         op("V", [("uq", 0, 128), ("uo", 0, 16)], [("pq", 0, 256)], lambda e: e.tensor_copy(T.pq[:, 0:256].bitcast(dt.uint32), T.uq[:, 0:128].bitcast(dt.uint32).indirect(T.uo[:, 0:16])))
-        tt(("e0", 0, C), ("e1", 0, C), ("jr", 0, C), OP.add)
-        quantx(0)
-        ts(("mask", 0, C), ("e0", 0, C), 1.0, OP.add)
-        quantx(1)
+        for j in range(2): quant("em", "ems", 128 * j, 128 * j + 128, ("eb", 3 - 2 * side - j, 515 - 2 * side - j))
+        for lo, hi in RUNS: quantx(lo, hi)
         scores(0)
         scores(1)
+        mate = T.cores[rank ^ STEP[0]]
+        send(mate, T.el[:, 0:256].bitcast(dt.uint8), T.em[:, 0:256].bitcast(dt.uint8), [("em", 0, 256)], "ae")
+        send(mate, T.els[:, 0:256], T.ems[:, 0:256], [("ems", 0, 256)], "ae")
+        note("ae", 2 * len(topo.engines(core, mate)), [], [("el", 0, 256), ("els", 0, 256)])
+        for k in range(3): iota(("qtab", k, F, 3), [[1, C]], C * k, 0, True)
+        cp(W0, ("k1", 0, 24))
 
-    ready1("om0", "w16", 0, first)
-    halves(0)
+    ready1("om0", "w16", 0, ("k1", 0, 24), ("k1", 24, 48), ("k1", 48, 72), first)
     ready2()
     signs(0)
+    tt(("du", 24, 48), W0, ("u0", 24, 48), OP.subtract)
+    tt(("du", 48, 72), ("u12", 0, 24), ("u0", 48, 72), OP.subtract)
     signs(1)
+    halves(0)
     halves(1)
 
     for k in range(ROUNDS):
@@ -312,75 +332,93 @@ def rank_program(g, core, T, topo):
         tt(z("sp"), z("mp"), z("p0"), OP.add)
         cp(z("p16"), z("sp"))
         move("A", ("pir", 1, F, 3), (("idr", 0, F), ("p16", 24, 48)))
-        move("A", ("pir", 2, F, 3), (("idr", 0, F), ("p16", 48, 72)))
+        move("A", ("pir", 2, 866, 3), (("idr", 0, F), ("p16", 48, 66)))
         for j in range(3): tt(("mu", 24 * j, 24 * j + 24), ("du", 24 * j, 24 * j + 24), f, OP.mult)
         tt(z("su"), z("mu"), z("u0"), OP.add)
         cp(z("u16"), z("su"))
         move("V", ("pir", 0, F, 3), (("idr", 0, F), ("p16", 0, 24)))
-        for q, j in (("V", 1), ("A", 2), ("A", 0)): move(q, (new, j, F, 3), (("pir", 0, F), ("u16", 24 * j, 24 * j + 24)))
+        move("V", ("pir", 866, F, 3), (("idr", 0, F), ("p16", 66, 72)))
+        for q, j in (("V", 1), ("A", 0), ("A", 2)): move(q, (new, j, F, 3), (("pir", 0, F), ("u16", 24 * j, 24 * j + 24)))
         scan(("sc", C, 2 * C), (new, 1, F, 3))
         agents(("l12", 0, 24), ends("sc", 1))
-        scan(("sc", 2 * C, 3 * C), (new, 2, F, 3))
-        agents(("l12", 24, 48), ends("sc", 2))
         scan(("sc", 0, C), (new, 0, F, 3))
         ports((dl, 0, 24), ends("sc", 0))
+        scan(("sc", 2 * C, 3 * C), (new, 2, F, 3))
+        agents(("l12", 24, 48), ends("sc", 2))
         send(peer, T[la][:, 0:24], T[dl][:, 0:24], [(dl, 0, 24)], "al%d" % k)
         note("al%d" % k, len(topo.engines(core, peer)), [], [(la, 0, 24)])
-        for i, (lo, hi) in enumerate(RUNS):
+        for i, (lo, hi) in enumerate(ZRUNS):
             for b in range(4): move("A", ("gz", C * b + lo, C * b + hi), (("xh", C * b, C * b + C), ("l12", lo // 16, hi // 16)))
-        for i, (lo, hi) in enumerate(RUNS):
+        if not last:
+            for j, w in enumerate((W0, W1, W2)): wraps(w, ends("sc", j))
+        for i, (lo, hi) in enumerate(ZRUNS):
             for b in range(4): tt(("zt", 4 * lo + b, 4 * hi, 4), (("xh", C * b, C * b + C), ("l12", 24 + lo // 16, 24 + hi // 16)), ("gz", C * b + lo, C * b + hi), OP.add)
             quant("zq", "zs", lo, hi, ("zt", 4 * lo, 4 * hi))
             for b in range(4): mm(4 * i + b, hi - lo, "wq", "wp", 128 * b, "zq", "zs", lo)
-        def places():
+        def look():
             move("A", ("mr", 0, C), ((new, 0, F), (la, 0, 24)))
+
+        def places():
             scan(("ms", 0, C), ("mr", 0, C))
             agents(("ml", 0, 24), ends("ms"))
-        for i, (lo, hi) in enumerate(RUNS):
-            if i == 1 and k > 0: places()
-            for q, b in (("V", 0), ("A", 1), ("V", 2), ("A", 3)): scaled(q, ("hp", C * b + lo, C * b + hi), psum(4 * i + b, hi - lo), 0.03125)
-        if k == 0: places()
-        for i, (lo, hi) in enumerate(RUNS):
-            hq, hs, lq, ls, n = "hq%d%d" % (k, i), "hs%d%d" % (k, i), "lq%d%d" % (k, i), "ls%d%d" % (k, i), hi - lo
+        for n, (q, i, b) in enumerate((("A", 0, 0), ("A", 0, 1), ("V", 0, 2), ("A", 0, 3), ("V", 1, 0), ("A", 1, 1), ("V", 1, 2), ("A", 1, 3))):
+            if n == 1: look()
+            if n == 3: places()
+            lo, hi = ZRUNS[i]
+            scaled(q, ("hp", C * b + lo, C * b + hi), psum(4 * i + b, hi - lo), 0.03125)
+        hq, hs, lq, ls = "hq%d" % k, "hs%d" % k, "lq%d" % k, "ls%d" % k
+        for i, (lo, hi) in enumerate(EXCHANGE[k]):
             for q, b in (("V", 0), ("A", 1), ("V", 2), ("A", 3)):
                 move(q, ("hg", 4 * lo + b, 4 * hi, 4), (("hp", C * b, C * b + C), ("ml", lo // 16, hi // 16)))
-            quant(hq, hs, 0, n, ("hg", 4 * lo, 4 * hi))
-            send(peer, T[lq][:, 0:n].bitcast(dt.uint8), T[hq][:, 0:n].bitcast(dt.uint8), [(hq, 0, n)], "ah%d%d" % (k, i))
-            send(peer, T[ls][:, 0:n], T[hs][:, 0:n], [(hs, 0, n)], "ah%d%d" % (k, i))
-            note("ah%d%d" % (k, i), 2 * len(topo.engines(core, peer)), [], [(lq, 0, n), (ls, 0, n)])
-        if k == 0:
-            for b in range(4): quant("eq", "es", 128 * b, 128 * b + 128, ("eb", 3 - b, 515 - b))
+            quant(hq, hs, lo, hi, ("hg", 4 * lo, 4 * hi))
+            send(peer, T[lq][:, lo:hi].bitcast(dt.uint8), T[hq][:, lo:hi].bitcast(dt.uint8), [(hq, lo, hi)], "ah%d%d" % (k, i))
+            send(peer, T[ls][:, lo:hi], T[hs][:, lo:hi], [(hs, lo, hi)], "ah%d%d" % (k, i))
+            note("ah%d%d" % (k, i), 2 * len(topo.engines(core, peer)), [], [(lq, lo, hi), (ls, lo, hi)])
         if k == 1: quant("vq", "vs", 0, 128, ("vt", 0, 512))
         if not last:
-            ports(W0, ends("sc", 0))
-            ports(W1, ends("sc", 1))
-            ports(W2, ends("sc", 2))
-            ready1(new, dl, 0)
+            ready1(new, dl, 0, W0, W1, W2)
             ready2()
         else:
             for j in range(3): ports(("fin", 24 * j, 24 * j + 24), ends("sc", j))
             move("A", ("owr", 0, F), (("qtab", 0, F), ("fin", 0, 72)))
             for j in range(8): dma("S", T.ow[j:j + 1, :], T.owr[16 * j:16 * j + 1, 0:F], [("owr", 0, F)], [])
-        for i, (lo, hi) in enumerate(RUNS):
-            for b in range(4): mm(4 - 4 * i + b, hi - lo, "eq", "es", 128 * b, "lq%d%d" % (k, i), "ls%d%d" % (k, i), 0)
-        for i, (lo, hi) in enumerate(RUNS):
+        def unpack(i):
+            lo, hi = EXCHANGE[k][i]
+            for b in range(4):
+                e, es = ("em", "ems") if b // 2 == side else ("el", "els")
+                mm(4 - 4 * (i % 2) + b, hi - lo, e, es, 128 * (b % 2), lq, ls, lo)
+
+        def add(i):
+            lo, hi = EXCHANGE[k][i]
             for b in range(4):
                 x = ("xt", 4 * lo + b, 4 * hi, 4)
-                tt(x, psum(4 - 4 * i + b, hi - lo), x, OP.add)
-            quantx(i)
-            if not last:
-                scores(i)
-                if i == 1:
-                    halves(0)
-                    signs(0)
-                    signs(1)
-                    halves(1)
-            else:
-                n = hi - lo
-                mm(4 - 4 * i, n, "vq", "vs", 0, "xq", "xs", lo)
-                dma("S", T.oc[:, 4 * lo:4 * hi], T.xq[:, lo:hi].bitcast(dt.uint8), [("xq", lo, hi)], [])
-                for j in range(4): dma("A" if j % 2 else "S", T.osc[4 * j:4 * j + 4, lo:hi], T.xs[32 * j:32 * j + 4, lo:hi], [("xs", lo, hi)], [])
-                ac(("yt", lo, hi), psum(4 - 4 * i, n))
-                dma("A", T.y[:, lo:hi], T.yt[:, lo:hi], [("yt", lo, hi)], [])
+                tt(x, psum(4 - 4 * (i % 2) + b, hi - lo), x, OP.add)
+            quantx(lo, hi)
+
+        def store(bank, lo, hi):
+            mm(bank, hi - lo, "vq", "vs", 0, "xq", "xs", lo)
+            dma("S", T.oc[:, 4 * lo:4 * hi], T.xq[:, lo:hi].bitcast(dt.uint8), [("xq", lo, hi)], [])
+            for j in range(4): dma("A" if j % 2 else "S", T.osc[4 * j:4 * j + 4, lo:hi], T.xs[32 * j:32 * j + 4, lo:hi], [("xs", lo, hi)], [])
+            ac(("yt", lo, hi), psum(bank, hi - lo))
+            dma("A", T.y[:, lo:hi], T.yt[:, lo:hi], [("yt", lo, hi)], [])
+        unpack(0)
+        unpack(1)
+        add(0)
+        if not last:
+            scores(0)
+            tt(("du", 24, 48), W0, ("u0", 24, 48), OP.subtract)
+            tt(("du", 48, 72), ("u12", 0, 24), ("u0", 48, 72), OP.subtract)
+            halves(0)
+            add(1)
+            scores(1)
+            signs(0, "A")
+            signs(1)
+            halves(1)
+        else:
+            unpack(2)
+            add(1)
+            store(0, 0, 256)
+            add(2)
+            store(1, 256, 384)
     for sem in ("V", "A", "P", "G", "left"): wait("G", sem, count[sem])
     for j in range(ndma[0]): wait("G", "d%d" % j, 16)

from concourse.mybir import dt, AluOpType, ActivationFunctionType as AF

OP = AluOpType
C = 384
F = 3 * C
K = 4194304.0
ROUNDS = 3
STEP = [1, 2, 3]
RUNS = [(0, 192), (192, 384)]
EXCHANGE = [RUNS, RUNS, [(0, 128), (128, 256), (256, 384)]]
ZRUNS = [(0, 256), (256, 384)]

SCRATCH = {
    "xt": ("sbuf", [128, 4 * C], "bfloat16"), "xh": ("sbuf", [128, 4 * C], "bfloat16"), "gz": ("sbuf", [128, 4 * C], "bfloat16"),
    "zt": ("sbuf", [128, 4 * C], "bfloat16"), "hp": ("sbuf", [128, 4 * C], "bfloat16"), "hg": ("sbuf", [128, 4 * C], "bfloat16"),
    "ut": ("sbuf", [128, 512], "bfloat16"), "vt": ("sbuf", [128, 512], "bfloat16"),
    "ones": ("sbuf", [128, F], "bfloat16"), "eb": ("sbuf", [128, 516], "bfloat16"),
    "uq": ("sbuf", [128, 128], "float8_e4m3fn_x4"), "us": ("sbuf", [128, 128], "uint8"),
    "pq": ("sbuf", [128, 256], "float8_e4m3fn_x4"), "psc": ("sbuf", [128, 256], "uint8"),
    "vq": ("sbuf", [128, 128], "float8_e4m3fn_x4"), "vs": ("sbuf", [128, 128], "uint8"),
    "em": ("sbuf", [128, 256], "float8_e4m3fn_x4"), "ems": ("sbuf", [128, 256], "uint8"), "el": ("sbuf", [128, 256], "float8_e4m3fn_x4"), "els": ("sbuf", [128, 256], "uint8"),
    "sg": ("sbuf", [128, 192], "float32"),
    "wq": ("sbuf", [128, 512], "float8_e4m3fn_x4"), "wp": ("sbuf", [128, 512], "uint8"),
    "xq": ("sbuf", [128, C], "float8_e4m3fn_x4"), "xs": ("sbuf", [128, C], "uint8"),
    "zq": ("sbuf", [128, C], "float8_e4m3fn_x4"), "zs": ("sbuf", [128, C], "uint8"),
    "wlt": ("sbuf", [128, 72], "int32"), "pi32": ("sbuf", [128, 1], "int32"), "p15i": ("sbuf", [128, 1], "int32"),
    "p15": ("sbuf", [128, 1], "float32"), "p3": ("sbuf", [128, 1], "float32"), "last": ("sbuf", [128, 1], "float32"),
    "inv": ("sbuf", [128, 1], "float32"), "inv3": ("sbuf", [128, 1], "float32"), "thp": ("sbuf", [128, 1], "float32"),
    "c48": ("sbuf", [128, 24], "float32"), "c3": ("sbuf", [128, 24], "float32"),
    "uoi": ("sbuf", [128, 16], "int32"), "uo": ("sbuf", [128, 16], "uint16"),
    "np15": ("sbuf", [128, 1], "float32"), "np16": ("sbuf", [128, 1], "float32"),
    "jr": ("sbuf", [128, 96], "float32"), "e0": ("sbuf", [128, 96], "float32"), "e1": ("sbuf", [128, 96], "float32"), "e2": ("sbuf", [128, 96], "float32"), "e3": ("sbuf", [128, 96], "float32"), "mask": ("sbuf", [128, C], "float32"),
    "idr": ("sbuf", [128, F], "float32"), "qtab": ("sbuf", [128, F], "float32"), "acttab": ("sbuf", [128, F], "bfloat16"),
    "pir": ("sbuf", [128, F], "float32"), "om0": ("sbuf", [128, F], "float32"), "om1": ("sbuf", [128, F], "float32"),
    "ew": ("sbuf", [128, 2 * C], "float32"), "hrow": ("sbuf", [128, C], "float32"), "thr": ("sbuf", [128, C], "float32"),
    "fr": ("sbuf", [128, C], "float32"), "fs": ("sbuf", [128, C], "float32"),
    "sc": ("sbuf", [128, F], "float32"), "y12": ("sbuf", [128, 2 * C], "float32"), "sy": ("sbuf", [128, 2 * C], "float32"),
    "mr": ("sbuf", [128, C], "float32"), "ms": ("sbuf", [128, C], "float32"), "ml": ("sbuf", [128, 24], "uint16"),
    "l12": ("sbuf", [128, 48], "uint16"),
    "q3": ("sbuf", [128, 72], "float32"), "k1": ("sbuf", [128, 72], "float32"), "k2": ("sbuf", [128, 72], "float32"), "kk": ("sbuf", [128, 72], "float32"),
    "u0": ("sbuf", [128, 72], "float32"), "du": ("sbuf", [128, 72], "float32"), "w12": ("sbuf", [128, 48], "float32"),
    "p0": ("sbuf", [128, 72], "float32"), "dp": ("sbuf", [128, 72], "float32"),
    "mp": ("sbuf", [128, 72], "float32"), "sp": ("sbuf", [128, 72], "float32"), "p16": ("sbuf", [128, 72], "uint16"),
    "mu": ("sbuf", [128, 72], "float32"), "su": ("sbuf", [128, 72], "float32"), "u16": ("sbuf", [128, 72], "uint16"),
    "ai": ("sbuf", [128, 24], "int32"), "a3": ("sbuf", [128, 24], "float32"), "act": ("sbuf", [128, 24], "float32"),
    "td": ("sbuf", [128, 24], "float32"), "ta": ("sbuf", [128, 24], "float32"), "tau": ("sbuf", [128, 24], "float32"),
    "ad0": ("sbuf", [128, 24], "float32"), "ad": ("sbuf", [128, 24], "float32"), "x12": ("sbuf", [128, 48], "uint16"),
    "a2m": ("sbuf", [128, 24], "float32"), "va": ("sbuf", [128, 24], "float32"), "vta": ("sbuf", [128, 24], "float32"), "ss": ("sbuf", [128, 24], "float32"),
    "u10": ("sbuf", [128, 24], "float32"), "u12": ("sbuf", [128, 24], "float32"), "dst": ("sbuf", [128, 24], "uint16"),
    "w16": ("sbuf", [128, 72], "uint16"), "fin": ("sbuf", [128, 72], "uint16"), "owr": ("sbuf", [128, F], "float32"), "yt": ("sbuf", [128, C], "float32"),
    "ps": ("psum", [128, 4096], "float32"),
}
for _k in range(ROUNDS):
    SCRATCH["dl%d" % _k] = ("sbuf", [128, 24], "uint16")
    SCRATCH["la%d" % _k] = ("sbuf", [128, 24], "uint16")
    for _n in ("h", "l"):
        SCRATCH["%sq%d" % (_n, _k)] = ("sbuf", [128, C], "float8_e4m3fn_x4")
        SCRATCH["%ss%d" % (_n, _k)] = ("sbuf", [128, C], "uint8")
SEMAPHORES = ["V", "A", "P", "G", "left", "ae"] + ["al%d" % k for k in range(ROUNDS)] + ["ah%d%d" % (k, i) for k in range(ROUNDS) for i in range(len(EXCHANGE[k]))] + ["d%d" % i for i in range(40)]


def rank_program(g, core, T, topo):
    rank = T.rank_of(core)
    if rank is None:
        return
    QUEUE = {"V": g.vector, "A": g.scalar, "P": g.tensor, "G": g, "S": g.sync}
    count = {}
    seen = {}
    book = {}

    def wait(q, sem, val):
        if seen.get((q, sem), 0) < val:
            QUEUE[q].wait_ge(T.sem[sem], val)
            seen[(q, sem)] = val

    def region(r):
        if len(r) == 3: return r[0], r[1], r[2], 1, 0
        return r[0], r[1], r[2], r[3], r[1] % r[3]

    def meets(a, b):
        if a[0] >= b[1] or b[0] >= a[1]: return False
        return not (a[2] == b[2] and a[3] != b[3])

    def note(sem, val, reads, writes):
        for r in reads:
            n, lo, hi, st, ph = region(r)
            book.setdefault(n, []).append((lo, hi, st, ph, sem, val, False))
        for r in writes:
            n, lo, hi, st, ph = region(r)
            l = [e for e in book.get(n, []) if not (lo <= e[0] and e[1] <= hi and (st == 1 or (st, ph) == (e[2], e[3])))]
            book[n] = l + [(lo, hi, st, ph, sem, val, True)]

    def depend(q, reads, writes):
        need = {}
        for rs, w in ((reads, False), (writes, True)):
            for r in rs:
                n, lo, hi, st, ph = region(r)
                for e in book.get(n, []):
                    if (w or e[6]) and meets((lo, hi, st, ph), e): need[e[4]] = max(need.get(e[4], 0), e[5])
        for sem in sorted(need): wait(q, sem, need[sem])

    def op(q, reads, writes, call):
        depend(q, reads, writes)
        count[q] = count.get(q, 0) + 1
        call(QUEUE[q]).then_inc(T.sem[q], 1)
        note(q, count[q], reads, writes)

    ndma = [0]

    def dma(q, out, in_, reads, writes):
        depend(q, reads, writes)
        sem = "d%d" % ndma[0]
        ndma[0] += 1
        count[sem] = 16
        QUEUE[q].dma_start(out, in_).then_inc(T.sem[sem], 16)
        note(sem, 16, reads, writes)

    def send(dst, out, in_, reads, sem):
        depend("G", reads, [])
        rid, pid, _ = topo.addr(dst)
        m = topo.mask(core, dst)
        count["left"] = count.get("left", 0) + len(topo.engines(core, dst))
        g.remote_dma(out, in_, T.sem[sem], T.sem.left, pid, rid, m)

    def ap(r):
        return T[r[0]][:, r[1]:r[2]] if len(r) == 3 else T[r[0]][:, r[1]:r[2]:r[3]]

    def apx(r):
        return (ap(r[0]).indirect(ap(r[1])), [r[0], r[1]]) if not isinstance(r[0], str) else (ap(r), [r])

    def tt(o, a, b, f):
        x, rd = apx(a)
        op("V", rd + [b], [o], lambda e: e.tensor_tensor(ap(o), x, ap(b), f))

    def ts(o, a, s1, f1, s2=None, f2=None, q="V"):
        x, rd = apx(a)
        rd = list(rd)
        if isinstance(s1, str):
            rd.append((s1, 0, 1))
            s1 = T[s1][:, 0:1]
        if f2 is None: op(q, rd, [o], lambda e: e.tensor_scalar(ap(o), x, s1, None, f1))
        else: op(q, rd, [o], lambda e: e.tensor_scalar(ap(o), x, s1, s2, f1, f2))

    def cp(o, a):
        x, rd = apx(a)
        op("V", rd, [o], lambda e: e.tensor_copy(ap(o), x))

    def ac(o, a, f=AF.Copy, scale=1.0, bias=0.0):
        x, rd = apx(a)
        rd = list(rd)
        arg = {}
        for n, s, plain in (("bias", bias, 0.0), ("scale", scale, 1.0)):
            if isinstance(s, str):
                rd.append((s, 0, 1))
                arg[n] = T[s][:, 0:1]
            elif s != plain: arg[n] = s
        op("A", rd, [o], lambda e: e.activation(ap(o), x, f, **arg))

    def move(q, o, a):
        (cp if q == "V" else ac)(o, a)

    def scaled(q, o, a, s):
        if q == "V": ts(o, a, s, OP.mult)
        else: ac(o, a, scale=s)

    def scan(o, a, f=OP.max):
        op("V", [("mask", 0, C), a], [o], lambda e: e.tensor_tensor_scan(ap(o), T.mask[:, 0:C], ap(a), 0.0, OP.mult, f))

    def quant(q, s, lo, hi, a):
        op("V", [a], [(q, lo, hi), (s, lo, hi)], lambda e: e.quantize_mx(T[q][:, lo:hi], T[s][:, lo:hi], ap(a)))

    def mm(bank, n, w, ws, wlo, x, xs, lo):
        op("P", [(w, wlo, wlo + 128), (ws, wlo, wlo + 128), (x, lo, lo + n), (xs, lo, lo + n)], [("ps", 512 * bank, 512 * bank + 512)],
           lambda e: e.matmul_mx(T.ps[:, 512 * bank:512 * bank + n], T[w][:, wlo:wlo + 128], T[ws][:, wlo:wlo + 128], T[x][:, lo:lo + n], T[xs][:, lo:lo + n], True, True))

    def psum(bank, n):
        return ("ps", 512 * bank, 512 * bank + n)

    def ends(b, i=0):
        return (b, C * i + 15, C * i + C, 16)

    def ports(o, s):
        ts(o, s, "inv", OP.mult, -1.0, OP.add)

    def wraps(o, s):
        ac(o, s, AF.Identity, scale="inv", bias=-1.0)

    def agents(o, s):
        ts(o, s, "inv3", OP.mult, -2.0 / 3.0, OP.add)

    dma("A", T.wlt[:, 0:72], T.wl[:, :], [], [("wlt", 0, 72)])
    dma("S", T.ut[:, 0:512], T.u[:, :], [], [("ut", 0, 512)])
    for i, (lo, hi) in enumerate(RUNS): dma("AS"[i], T.xt[:, 4 * lo:4 * hi], T.x[:, 4 * lo:4 * hi], [], [("xt", 4 * lo, 4 * hi)])
    dma("S", T.wq[:, 0:512].bitcast(dt.uint8), T.wc[:, :], [], [("wq", 0, 512)])
    dma("S", T.wp[:, 0:512], T.ws[:, :], [], [("wp", 0, 512)])
    dma("S", T.vt[:, 0:512], T.v[:, :], [], [("vt", 0, 512)])

    def iota(r, pattern, base, mult, flag):
        op("G", [], [r], lambda e: e.iota(ap(r), pattern, base, mult, allow_small_or_imprecise_dtypes=True) if flag else e.iota(ap(r), pattern, base, mult))
    iota(("pi32", 0, 1), [[0, 1]], 0, 1, False)
    iota(("c48", 0, 24), [[48, 24]], 0, 0, True)
    iota(("uoi", 0, 16), [[1, 2], [16, 8]], 0, 0, False)
    iota(("jr", 0, 96), [[0, 6], [1, 16]], 0, 0, True)
    side = 0 if rank < (rank ^ STEP[0]) else 1
    op("V", [], [("ones", 0, F)], lambda e: e.memset(T.ones[:, 0:F], 1.0))
    for j in range(3): ac(("acttab", j, F, 3), ("ones", 0, C), scale=-1e29 if j else 0.0)
    ts(("p15i", 0, 1), ("pi32", 0, 1), 15, OP.bitwise_and)
    cp(("p15", 0, 1), ("p15i", 0, 1))
    ts(("np15", 0, 1), ("p15", 0, 1), -1.0, OP.mult)
    ts(("np16", 0, 1), ("p15", 0, 1), -1.0, OP.mult, -1.0, OP.add)
    ac(("e0", 0, 96), ("jr", 0, 96), AF.Sign, bias="np15")
    ac(("e1", 0, 96), ("jr", 0, 96), AF.Abs, bias="np16")
    ac(("e2", 0, 96), ("e0", 0, 96), AF.Abs)
    ac(("e3", 0, 96), ("e1", 0, 96), AF.Relu, scale=-K, bias=K)
    op("V", [("ones", 0, F)], [("idr", 0, F)], lambda e: e.tensor_tensor_scan(T.idr[:, 0:F], T.ones[:, 0:F], T.ones[:, 0:F], 0.0, OP.mult, OP.add))
    op("G", [("ones", 0, 516)], [("eb", 0, 516)], lambda e: e.affine_select(T.eb[:, 0:516], T.ones[:, 0:516], [[-1, 516]], OP.is_equal, 0.0, 3, 4))
    cp(("uo", 0, 16), ("uoi", 0, 16))
    ts(("p3", 0, 1), ("p15", 0, 1), 3.0, OP.mult)
    ts(("last", 0, 1), ("p15", 0, 1), 15.0, OP.is_equal)
    ts(("c3", 0, 24), ("c48", 0, 24), "p3", OP.add)
    ts(("inv", 0, 1), ("last", 0, 1), 1.0 - 1.0 / K, OP.mult, 1.0 / K, OP.add)
    ts(("thp", 0, 1), ("last", 0, 1), 1.0 - K, OP.mult, K, OP.add)
    ts(("inv3", 0, 1), ("inv", 0, 1), 1.0 / 3.0, OP.mult)
    cp(("p0", 0, 24), ("c3", 0, 24))
    tt(("mask", 0, 96), ("e2", 0, 96), ("e3", 0, 96), OP.max)
    ac(("mask", 96, 192), ("mask", 0, 96))
    ac(("mask", 192, C), ("mask", 0, 192))

    w72 = ("wlt", 0, 72)
    ts(("k1", 0, 72), w72, 384.0, OP.is_ge, -1151.0, OP.mult)
    ts(("k2", 0, 72), w72, 768.0, OP.is_ge, -1151.0, OP.mult)
    ts(("q3", 0, 72), w72, 3.0, OP.mult)
    tt(("kk", 0, 72), ("k1", 0, 72), ("k2", 0, 72), OP.add)
    tt(("k1", 0, 72), ("q3", 0, 72), ("kk", 0, 72), OP.add)
    cp(("w16", 0, 72), ("k1", 0, 72))
    move("A", ("om0", 1, F, 3), (("idr", 0, F), ("w16", 24, 48)))
    move("A", ("om0", 2, F, 3), (("idr", 0, F), ("w16", 48, 72)))
    move("V", ("om0", 0, F, 3), (("idr", 0, F), ("w16", 0, 24)))

    W0, W1, W2 = ("u0", 0, 24), ("w12", 0, 24), ("w12", 24, 48)

    def ready1(om, lst, loff, W0, W1, W2, meanwhile=None):
        z = lambda n: (n, 0, 24)
        ts(z("ai"), W0, 1.0 / 3.0, OP.mult, -1.0 / 3.0, OP.add)
        tt(z("td"), W0, z("c3"), OP.subtract)
        tt(z("ad0"), W2, W1, OP.subtract)
        ts(z("a3"), z("ai"), 3.0, OP.mult)
        tt(z("act"), W0, z("a3"), OP.is_equal)
        if not meanwhile: move("A", ("thr", 0, C), (("acttab", 0, F), (lst, loff, loff + 24)))
        tt(z("ta"), z("td"), z("act"), OP.mult)
        tt(z("tau"), z("ta"), z("c3"), OP.add)
        ts(("p0", 24, 48), z("tau"), 1.0, OP.add)
        ts(("p0", 48, 72), z("tau"), 2.0, OP.add)
        cp(("x12", 0, 48), ("p0", 24, 72))
        if meanwhile: meanwhile()
        ac(z("va"), z("act"), AF.Identity, scale=-1152.0, bias=1152.0)
        ac(z("a2m"), z("act"), AF.Identity, scale=2.0, bias=-1.0)
        move("A", ("y12", 0, C), ((om, 0, F), ("x12", 0, 24)))
        move("A", ("y12", C, 2 * C), ((om, 0, F), ("x12", 24, 48)))
        if meanwhile: move("A", ("thr", 0, C), (("acttab", 0, F), (lst, loff, loff + 24)))
        tt(z("ad"), z("ad0"), z("act"), OP.mult)
        tt(z("vta"), z("va"), z("tau"), OP.add)
        tt(z("ss"), z("a2m"), z("ta"), OP.add)
        ts(z("dst"), z("vta"), 1.0 / 3.0, OP.mult)
        tt(("dp", 24, 48), z("a2m"), z("ta"), OP.subtract)
        ac(("dp", 48, 72), z("ss"), AF.Identity, scale=-1.0, bias=-1.0)
        tt(z("u10"), W1, z("ad"), OP.add)
        tt(z("u12"), W2, z("ad"), OP.subtract)
        tt(("du", 0, 24), z("u10"), W0, OP.subtract)

    def ready2():
        scan(("sy", 0, C), ("y12", 0, C))
        scan(("sy", C, 2 * C), ("y12", C, 2 * C))
        for j in range(2): wraps(("u0", 24 + 24 * j, 48 + 24 * j), ends("sy", j))

    def quantx(lo, hi):
        quant("xq", "xs", lo, hi, ("xt", 4 * lo, 4 * hi))

    def scores(i):
        lo, hi = RUNS[i]
        mm(4 - 4 * i, hi - lo, "pq", "psc", 0, "xq", "xs", lo)
        mm(5 - 4 * i, hi - lo, "pq", "psc", 128, "xq", "xs", lo)

    def signs(i, q="V"):
        lo, hi = RUNS[i]
        n = hi - lo
        if q == "V": ts(("ew", lo, hi), psum(4 - 4 * i, n), 0.0, OP.is_gt)
        else:
            op("A", [], [("sg", 0, n), psum(4 - 4 * i, n)], lambda e: e.activation(T.sg[:, 0:n], ap(psum(4 - 4 * i, n)), AF.Sign))
            ac(("ew", lo, hi), ("sg", 0, n), AF.Relu)
        ac(("ew", C + lo, C + hi), psum(5 - 4 * i, n), AF.Sign)
        tt(("hrow", lo, hi), psum(4 - 4 * i, n), ("thr", lo, hi), OP.is_gt)

    def halves(i):
        lo, hi = RUNS[i]
        for b in range(4): ac(("xh", C * b + lo, C * b + hi), ("xt", 4 * lo + b, 4 * hi, 4), scale=0.5)

    def first():
        quant("uq", "us", 0, 128, ("ut", 0, 512))
        op("A", [("us", 0, 128), ("uo", 0, 16)], [("psc", 0, 256)], lambda e: e.activation(T.psc[:, 0:256], T.us[:, 0:128].indirect(T.uo[:, 0:16]), AF.Copy))
        op("V", [("uq", 0, 128), ("uo", 0, 16)], [("pq", 0, 256)], lambda e: e.tensor_copy(T.pq[:, 0:256].bitcast(dt.uint32), T.uq[:, 0:128].bitcast(dt.uint32).indirect(T.uo[:, 0:16])))
        for j in range(2): quant("em", "ems", 128 * j, 128 * j + 128, ("eb", 3 - 2 * side - j, 515 - 2 * side - j))
        for lo, hi in RUNS: quantx(lo, hi)
        scores(0)
        scores(1)
        mate = T.cores[rank ^ STEP[0]]
        send(mate, T.el[:, 0:256].bitcast(dt.uint8), T.em[:, 0:256].bitcast(dt.uint8), [("em", 0, 256)], "ae")
        send(mate, T.els[:, 0:256], T.ems[:, 0:256], [("ems", 0, 256)], "ae")
        note("ae", 2 * len(topo.engines(core, mate)), [], [("el", 0, 256), ("els", 0, 256)])
        for k in range(3): iota(("qtab", k, F, 3), [[1, C]], C * k, 0, True)
        cp(W0, ("k1", 0, 24))

    ready1("om0", "w16", 0, ("k1", 0, 24), ("k1", 24, 48), ("k1", 48, 72), first)
    ready2()
    signs(0)
    tt(("du", 24, 48), W0, ("u0", 24, 48), OP.subtract)
    tt(("du", 48, 72), ("u12", 0, 24), ("u0", 48, 72), OP.subtract)
    signs(1)
    halves(0)
    halves(1)

    for k in range(ROUNDS):
        old, new = ("om0", "om1") if k % 2 == 0 else ("om1", "om0")
        peer = T.cores[rank ^ STEP[k]]
        dl, la, last = "dl%d" % k, "la%d" % k, k == ROUNDS - 1
        tt(("fr", 0, C), (("ew", 0, 2 * C), ("dst", 0, 24)), ("hrow", 0, C), OP.is_equal)
        scan(("fs", 0, C), ("fr", 0, C), OP.add)
        z = lambda n: (n, 0, 72)
        f = ("mp", 0, 24)
        ts(f, ends("fs"), "thp", OP.is_ge)
        for j in (1, 2): tt(("mp", 24 * j, 24 * j + 24), ("dp", 24 * j, 24 * j + 24), f, OP.mult)
        tt(z("sp"), z("mp"), z("p0"), OP.add)
        cp(z("p16"), z("sp"))
        move("A", ("pir", 1, F, 3), (("idr", 0, F), ("p16", 24, 48)))
        move("A", ("pir", 2, 866, 3), (("idr", 0, F), ("p16", 48, 66)))
        for j in range(3): tt(("mu", 24 * j, 24 * j + 24), ("du", 24 * j, 24 * j + 24), f, OP.mult)
        tt(z("su"), z("mu"), z("u0"), OP.add)
        cp(z("u16"), z("su"))
        move("V", ("pir", 0, F, 3), (("idr", 0, F), ("p16", 0, 24)))
        move("V", ("pir", 866, F, 3), (("idr", 0, F), ("p16", 66, 72)))
        for q, j in (("V", 1), ("A", 0), ("A", 2)): move(q, (new, j, F, 3), (("pir", 0, F), ("u16", 24 * j, 24 * j + 24)))
        scan(("sc", C, 2 * C), (new, 1, F, 3))
        agents(("l12", 0, 24), ends("sc", 1))
        scan(("sc", 0, C), (new, 0, F, 3))
        ports((dl, 0, 24), ends("sc", 0))
        scan(("sc", 2 * C, 3 * C), (new, 2, F, 3))
        agents(("l12", 24, 48), ends("sc", 2))
        send(peer, T[la][:, 0:24], T[dl][:, 0:24], [(dl, 0, 24)], "al%d" % k)
        note("al%d" % k, len(topo.engines(core, peer)), [], [(la, 0, 24)])
        for i, (lo, hi) in enumerate(ZRUNS):
            for b in range(4): move("A", ("gz", C * b + lo, C * b + hi), (("xh", C * b, C * b + C), ("l12", lo // 16, hi // 16)))
        if not last:
            for j, w in enumerate((W0, W1, W2)): wraps(w, ends("sc", j))
        for i, (lo, hi) in enumerate(ZRUNS):
            for b in range(4): tt(("zt", 4 * lo + b, 4 * hi, 4), (("xh", C * b, C * b + C), ("l12", 24 + lo // 16, 24 + hi // 16)), ("gz", C * b + lo, C * b + hi), OP.add)
            quant("zq", "zs", lo, hi, ("zt", 4 * lo, 4 * hi))
            for b in range(4): mm(4 * i + b, hi - lo, "wq", "wp", 128 * b, "zq", "zs", lo)
        def look():
            move("A", ("mr", 0, C), ((new, 0, F), (la, 0, 24)))

        def places():
            scan(("ms", 0, C), ("mr", 0, C))
            agents(("ml", 0, 24), ends("ms"))
        for n, (q, i, b) in enumerate((("A", 0, 0), ("A", 0, 1), ("V", 0, 2), ("A", 0, 3), ("V", 1, 0), ("A", 1, 1), ("V", 1, 2), ("A", 1, 3))):
            if n == 1: look()
            if n == 3: places()
            lo, hi = ZRUNS[i]
            scaled(q, ("hp", C * b + lo, C * b + hi), psum(4 * i + b, hi - lo), 0.03125)
        hq, hs, lq, ls = "hq%d" % k, "hs%d" % k, "lq%d" % k, "ls%d" % k
        for i, (lo, hi) in enumerate(EXCHANGE[k]):
            for q, b in (("V", 0), ("A", 1), ("V", 2), ("A", 3)):
                move(q, ("hg", 4 * lo + b, 4 * hi, 4), (("hp", C * b, C * b + C), ("ml", lo // 16, hi // 16)))
            quant(hq, hs, lo, hi, ("hg", 4 * lo, 4 * hi))
            send(peer, T[lq][:, lo:hi].bitcast(dt.uint8), T[hq][:, lo:hi].bitcast(dt.uint8), [(hq, lo, hi)], "ah%d%d" % (k, i))
            send(peer, T[ls][:, lo:hi], T[hs][:, lo:hi], [(hs, lo, hi)], "ah%d%d" % (k, i))
            note("ah%d%d" % (k, i), 2 * len(topo.engines(core, peer)), [], [(lq, lo, hi), (ls, lo, hi)])
        if k == 1: quant("vq", "vs", 0, 128, ("vt", 0, 512))
        if not last:
            ready1(new, dl, 0, W0, W1, W2)
            ready2()
        else:
            for j in range(3): ports(("fin", 24 * j, 24 * j + 24), ends("sc", j))
            move("A", ("owr", 0, F), (("qtab", 0, F), ("fin", 0, 72)))
            for j in range(8): dma("S", T.ow[j:j + 1, :], T.owr[16 * j:16 * j + 1, 0:F], [("owr", 0, F)], [])
        def unpack(i):
            lo, hi = EXCHANGE[k][i]
            for b in range(4):
                e, es = ("em", "ems") if b // 2 == side else ("el", "els")
                mm(4 - 4 * (i % 2) + b, hi - lo, e, es, 128 * (b % 2), lq, ls, lo)

        def add(i):
            lo, hi = EXCHANGE[k][i]
            for b in range(4):
                x = ("xt", 4 * lo + b, 4 * hi, 4)
                tt(x, psum(4 - 4 * (i % 2) + b, hi - lo), x, OP.add)
            quantx(lo, hi)

        def store(bank, lo, hi):
            mm(bank, hi - lo, "vq", "vs", 0, "xq", "xs", lo)
            dma("S", T.oc[:, 4 * lo:4 * hi], T.xq[:, lo:hi].bitcast(dt.uint8), [("xq", lo, hi)], [])
            for j in range(4): dma("A" if j % 2 else "S", T.osc[4 * j:4 * j + 4, lo:hi], T.xs[32 * j:32 * j + 4, lo:hi], [("xs", lo, hi)], [])
            ac(("yt", lo, hi), psum(bank, hi - lo))
            dma("A", T.y[:, lo:hi], T.yt[:, lo:hi], [("yt", lo, hi)], [])
        unpack(0)
        unpack(1)
        add(0)
        if not last:
            scores(0)
            tt(("du", 24, 48), W0, ("u0", 24, 48), OP.subtract)
            tt(("du", 48, 72), ("u12", 0, 24), ("u0", 48, 72), OP.subtract)
            halves(0)
            add(1)
            scores(1)
            signs(0, "A")
            signs(1)
            halves(1)
        else:
            unpack(2)
            add(1)
            store(0, 0, 256)
            add(2)
            store(1, 256, 384)
    for sem in ("V", "A", "P", "G", "left"): wait("G", sem, count[sem])
    for j in range(ndma[0]): wait("G", "d%d" % j, 16)
